import numpy as np
import ml_dtypes


def mxq(x, axis, fmt="e4m3"):
    dtype, down = {"e4m3": (ml_dtypes.float8_e4m3fn, 7), "e5m2": (ml_dtypes.float8_e5m2, 14)}[fmt]
    v = np.moveaxis(np.asarray(x, np.float32).astype(ml_dtypes.bfloat16).astype(np.float64), axis, -1)
    blocks = v.reshape(v.shape[:-1] + (-1, 32))
    amax = np.abs(blocks).max(-1, keepdims=True)
    byte = np.maximum(np.where(amax > 0, np.frexp(amax)[1] - 1 + 127, 0) - down, 1)
    scale = np.exp2(byte - 127.0)
    codes = (blocks / scale).astype(np.float32).astype(dtype).astype(np.float64)
    return np.moveaxis((codes * scale).reshape(v.shape), -1, axis)


WIDE = False


def mx_kscale(k):
    if not WIDE:
        return np.ones(k)
    levels = np.array([10, -10, 5, -5, 0])
    if k % 512:
        return np.exp2(np.random.permutation(np.resize(levels, k // 32))).repeat(32)
    a = np.empty((k // 512, 16))
    for p in range(k // 512):
        a[p, :8] = np.random.permutation(np.resize(levels, 8))
        for g in range(8):
            far = levels[np.abs(levels - a[p, g]) >= 10]
            a[p, g + 8] = far[np.random.randint(len(far))]
    return np.exp2(a.ravel()).repeat(32)


def f64(x):
    return np.asarray(x).astype(np.float64)


def striped8(idx):
    return np.asarray(idx).reshape(8, -1, 16).transpose(0, 2, 1).reshape(128, -1).astype(np.uint16)


def unstriped8(offs):
    return offs.reshape(8, 16, -1).transpose(0, 2, 1).reshape(8, -1).astype(np.int64)


def pick8(x, idx, run):
    r = np.arange(len(x))
    return x[r[:, None], idx[r % (8 * run) // run]]


E2M1 = np.array([0.0, 0.5, 1.0, 1.5, 2.0, 3.0, 4.0, 6.0, -0.0, -0.5, -1.0, -1.5, -2.0, -3.0, -4.0, -6.0])


def pack_weight(w, fmt):
    k, n = w.shape
    w = f64(np.asarray(w, np.float32).astype(ml_dtypes.bfloat16)).reshape(k // 32, 32, n)
    amax = np.abs(w).max(1)
    if fmt == "e4m3":
        byte = np.frexp(amax)[1] - 1 + 127 - 7
    else:
        mant, ex = np.frexp(amax / 6.0)
        byte = np.where(mant > 0.5, ex, ex - 1) + 127
    byte = np.clip(np.where(amax > 0, byte, 1), 1, 254)
    scaled = (w * np.exp2(127.0 - byte)[:, None, :]).reshape(k, n).astype(np.float32)
    by_word = np.ascontiguousarray(scaled.reshape(k // 512, 128, 4, n).transpose(0, 1, 3, 2))
    if fmt == "e4m3":
        words = by_word.astype(ml_dtypes.float8_e4m3fn).view(np.uint8)
    else:
        c = by_word.astype(ml_dtypes.float4_e2m1fn).view(np.uint8) & 0xF
        words = (c[..., 0::2] | (c[..., 1::2] << 4)).reshape(k // 512, 128, 2 * n)
    return np.ascontiguousarray(words), np.ascontiguousarray(byte.astype(np.uint8).reshape(k // 512, 16, n))


def unpack_weight(words, scales, fmt):
    g, _, n = scales.shape
    words = np.ascontiguousarray(words).reshape(g, 128, n, -1)
    if fmt == "e4m3":
        vals = words.view(ml_dtypes.float8_e4m3fn).astype(np.float64)
    else:
        nib = np.empty((g, 128, n, 4), np.uint8)
        nib[..., 0::2] = words & 0xF
        nib[..., 1::2] = words >> 4
        vals = E2M1[nib]
    vals = vals * np.repeat(np.exp2(scales.astype(np.float64) - 127.0), 8, axis=1)[..., None]
    return vals.transpose(0, 1, 3, 2).reshape(g * 512, n)


D, T, Q, I, E = 512, 1024, 128, 512, 512


def setup_inputs():
    n = np.random.standard_normal
    idx = np.stack([np.random.permutation(T)[:I] for _ in range(8)])
    fd = mx_kscale(D)
    ft = mx_kscale(T)
    keysp = pack_weight(n((D, T)) / fd[:, None], "e2m1")
    return {
        "query": (n((D, Q)) * 0.25 / np.sqrt(D) * fd[:, None]).astype(np.float32),
        "keys_words": keysp[0],
        "keys_scales": keysp[1],
        "pos": np.tile(np.random.uniform(0.0, 1.0, T), (128, 1)).astype(np.float32),
        "qpos": (np.random.uniform(0.2, 1.2, (Q, 1))).astype(np.float32),
        "slope": (np.random.uniform(0.2, 0.8, (Q, 1))).astype(np.float32),
        "fac": (np.random.uniform(4.0, 16.0, (1, T)) * ft).astype(np.float32),
        "vals": (n((T, E)) / ft[:, None]).astype(np.float32),
        "offs": striped8(idx),
    }


def reference(query, keys_words, keys_scales, pos, qpos, slope, fac, vals, offs):
    idx = unstriped8(offs)
    keysu = unpack_weight(keys_words, keys_scales, "e2m1")
    queryq = mxq(f64(query), 0, "e4m3")
    a = queryq.T @ keysu
    s = pick8(a, idx, 16) - f64(slope) * np.square(f64(qpos) - pick8(f64(pos), idx, 16))
    p = np.exp(s - np.max(s, axis=1, keepdims=True))
    w = p / np.sum(p, axis=1, keepdims=True)
    wf = np.zeros((Q, T))
    wf[np.arange(Q)[:, None], idx[np.arange(Q) % 128 // 16]] = w
    wg = wf * f64(fac)
    wt = wg.T
    wtq = mxq(wt, 0, "e4m3")
    valsq = mxq(f64(vals), 0, "e4m3")
    o = wtq.T @ valsq
    return o

@@ -1,0 +1,212 @@
+from contextlib import ExitStack
+
+import concourse.mybir as mybir
+from concourse.masks import make_identity
+
+D, T, Q, I, E = 512, 1024, 128, 512, 512
+FLOPS = 2 * D * T * Q + 2 * T * Q * E
+
+F32 = mybir.dt.float32
+BF16 = mybir.dt.bfloat16
+I32 = mybir.dt.int32
+U32 = mybir.dt.uint32
+U16 = mybir.dt.uint16
+U8 = mybir.dt.uint8
+FP8X4 = mybir.dt.float8_e4m3fn_x4
+FP4X4 = mybir.dt.float4_e2m1fn_x4
+ALU = mybir.AluOpType
+ACT = mybir.ActivationFunctionType
+AXIS = mybir.AxisListType
+
+P = 128
+PACK = 4
+K_PASS = P * PACK
+BANK = 512
+HALF = 256
+HEAD = 128
+
+
+def tile_attend_ownlists_positions_kernel(
+    tc, query, keys_words, keys_scales, pos, qpos, slope, fac, vals, offs, out
+):
+    nc = tc.nc
+    passes = T // K_PASS
+
+    with ExitStack() as ctx:
+        keep = ctx.enter_context(tc.tile_pool(name="keep", bufs=1))
+        psum = ctx.enter_context(tc.psum_pool(name="psum", bufs=1))
+
+        k_scales = keep.tile([P, T], U8, align_bytes=64)
+        warm = keep.tile([P, 1], F32)
+        nc.vector.memset(warm[:], 0.0)
+        warm_out = keep.tile([P, 1], F32)
+        nc.scalar.activation(warm_out[:], warm[:], ACT.Exp)
+
+        q_raw = keep.tile([P, PACK, Q], F32)
+        nc.sync.dma_start(out=q_raw[:], in_=query.rearrange("(p j) q -> p j q", j=PACK))
+        for quad in range(4):
+            nc.scalar.dma_start(
+                out=k_scales[32 * quad : 32 * quad + 4, :].bitcast(I32),
+                in_=keys_scales[0, 4 * quad : 4 * quad + 4, :].bitcast(I32),
+            )
+        offsets = keep.tile([P, I // 16], U16)
+        nc.sync.dma_start(offsets[:], offs)
+        pos_all = keep.tile([P, T], F32)
+        nc.sync.dma_start(out=pos_all[:], in_=pos)
+        k_words = keep.tile([P, 2 * T], U8, align_bytes=64)
+        nc.sync.dma_start(out=k_words[:].bitcast(I32), in_=keys_words[0].bitcast(I32))
+        qpos_col = keep.tile([P, 1], F32)
+        nc.sync.dma_start(out=qpos_col[:], in_=qpos)
+        slope_col = keep.tile([P, 1], F32)
+        nc.sync.dma_start(out=slope_col[:], in_=slope)
+        fac_cols = keep.tile([P, passes, PACK], F32)
+        nc.sync.dma_start(out=fac_cols[:], in_=fac.rearrange("o (g p j) -> p (o g) j", g=passes, j=PACK))
+        v_raw = []
+        for g in range(passes):
+            tile_g = keep.tile([P, PACK, E], F32, name=f"v_raw{g}", tag=f"v_raw{g}", align_bytes=64)
+            nc.sync.dma_start(
+                out=tile_g[:],
+                in_=vals[g * K_PASS : (g + 1) * K_PASS, :].rearrange("(p j) e -> p j e", j=PACK),
+            )
+            v_raw.append(tile_g)
+
+        ident = keep.tile([P, P], F32)
+        make_identity(nc, ident[:])
+        w_full = keep.tile([P, T], F32)
+        nc.gpsimd.memset(w_full[:], 0.0)
+
+        q_bf = keep.tile([P, Q, PACK], BF16, align_bytes=64)
+        nc.vector.tensor_copy(out=q_bf[:], in_=q_raw[:].rearrange("p j q -> p q j"))
+        q_codes = keep.tile([P, Q], U32, align_bytes=64)
+        q_scales = keep.tile([P, Q], U8, align_bytes=64)
+        nc.vector.quantize_mx(
+            out=q_codes[:].bitcast(FP8X4), scales=q_scales[:], in_=q_bf[:].rearrange("p q j -> p (q j)")
+        )
+
+        pos_listed = keep.tile([P, I], F32)
+        dist2 = keep.tile([P, I], F32)
+        penalty = keep.tile([P, I], F32)
+        for h in range(2):
+            slots = slice(h * HALF, (h + 1) * HALF)
+            nc.vector.tensor_copy(
+                pos_listed[:, slots], pos_all[:].indirect(offsets[:, h * HALF // 16 : (h + 1) * HALF // 16])
+            )
+            nc.scalar.activation(dist2[:, slots], pos_listed[:, slots], ACT.Square, bias=qpos_col[:], scale=-1.0)
+            nc.scalar.activation(penalty[:, slots], dist2[:, slots], ACT.Copy, scale=slope_col[:])
+
+        scores = keep.tile([P, T], F32)
+        for h in range(T // HALF):
+            cols = slice(h * HALF, (h + 1) * HALF)
+            bank = psum.tile([P, HALF], F32, name=f"score_bank{h}", tag=f"bank{h}")
+            nc.tensor.matmul_mx(
+                out=bank[:],
+                lhsT=q_codes[:].bitcast(FP8X4),
+                lhsT_scale=q_scales[:],
+                rhs=k_words[:, 2 * h * HALF : 2 * (h + 1) * HALF].bitcast(FP4X4),
+                rhs_scale=k_scales[:, cols],
+                start=True,
+                stop=True,
+            )
+            if h < T // HALF - 1:
+                nc.vector.tensor_copy(out=scores[:, cols], in_=bank[:])
+            else:
+                nc.scalar.copy(out=scores[:, cols], in_=bank[:])
+
+        fac_banks = []
+        for g in range(passes):
+            fac_bank = psum.tile([P, PACK, P], F32, name=f"fac_bank{g}")
+            for j in range(PACK):
+                nc.tensor.transpose(fac_bank[:, j, :], fac_cols[:, g, j : j + 1].to_broadcast([P, P]), ident[:])
+            fac_banks.append(fac_bank)
+
+        v_bf = {}
+        v_codes = [keep.tile([P, E], U32, align_bytes=64, name=f"v_codes{g}") for g in range(passes)]
+        v_scales = [keep.tile([P, E], U8, align_bytes=64, name=f"v_scales{g}") for g in range(passes)]
+
+        def cast_values(g, c0, c1, tag):
+            v_bf[g, c0] = keep.tile([P, c1 - c0, PACK], BF16, align_bytes=64, name=f"v_bf{g}_{c0}", tag=tag)
+            nc.scalar.copy(
+                out=v_bf[g, c0][:].rearrange("p (c i) j -> p c j i", i=4),
+                in_=v_raw[g][:, :, c0:c1].rearrange("p j (c i) -> p c j i", i=4),
+            )
+
+        def quantise_values(g, c0, c1):
+            nc.vector.quantize_mx(
+                out=v_codes[g][:, c0:c1].bitcast(FP8X4),
+                scales=v_scales[g][:, c0:c1],
+                in_=v_bf[g, c0][:].rearrange("p e j -> p (e j)"),
+            )
+
+        s = keep.tile([P, I], F32, align_bytes=64, tag="shared")
+        nc.vector.tensor_tensor(s[:], scores[:].indirect(offsets[:]), penalty[:], ALU.subtract)
+        neg_max = keep.tile([P, 1], F32)
+        nc.vector.tensor_reduce(neg_max[:], s[:], AXIS.X, ALU.max, negate=True)
+        cast_values(0, 0, HALF, "v_bf_a")
+        p_head = v_raw[0][:, 0, :HEAD]
+        nc.scalar.activation(p_head, s[:, :HEAD], ACT.Exp, bias=neg_max[:])
+        p_all = keep.tile([P, I], F32)
+        row_sum = keep.tile([P, 1], F32)
+        nc.scalar.activation(p_all[:], s[:], ACT.Exp, bias=neg_max[:], accum_out=row_sum[:])
+        quantise_values(0, 0, HALF)
+        nc.vector.tensor_copy(w_full[:].indirect(offsets[:, : HEAD // 16]), p_head)
+        inv_sum = keep.tile([P, 1], F32)
+        nc.vector.reciprocal(inv_sum[:], row_sum[:])
+        nc.vector.tensor_copy(w_full[:].indirect(offsets[:, HEAD // 16 :]), p_all[:, HEAD:])
+        cast_values(0, HALF, E, "shared")
+        cast_values(1, 0, HALF, "v_bf_b")
+        cast_values(1, HALF, E, "v_bf_c")
+        quantise_values(0, HALF, E)
+
+        w_t = []
+        for g in range(passes):
+            w_bf = keep.tile([P, K_PASS], BF16, align_bytes=64, name=f"w_bf{g}", tag=("shared", "w_bf")[g])
+            nc.vector.scalar_tensor_tensor(
+                out=w_bf[:].rearrange("q (p j) -> q p j", j=PACK),
+                in0=w_full[:, g * K_PASS : (g + 1) * K_PASS].rearrange("q (p j) -> q p j", j=PACK),
+                scalar=inv_sum[:],
+                in1=fac_banks[g][:].rearrange("q j p -> q p j"),
+                op0=ALU.mult,
+                op1=ALU.mult,
+            )
+            pairs = w_bf[:].bitcast(F32)
+            turned = psum.tile([P, 2, Q], F32, name=f"turned{g}", tag=f"bank{g}")
+            for u in range(2):
+                nc.tensor.transpose(turned[:, u, :], pairs[:, u : K_PASS // 2 : 2], ident[:])
+            w_tg = keep.tile([P, Q * PACK], BF16, align_bytes=64, name=f"w_t{g}", tag=f"v_raw{1 - g}")
+            nc.scalar.copy(
+                out=w_tg[:].bitcast(F32).rearrange("p (q u) -> p q u", u=2),
+                in_=turned[:].rearrange("p u q -> p q u"),
+            )
+            w_t.append(w_tg)
+
+        quantise_values(1, 0, HALF)
+        quantise_values(1, HALF, E)
+
+        w_codes = []
+        w_scales = []
+        for g in range(passes):
+            codes = keep.tile([P, Q], U32, align_bytes=64, name=f"w_codes{g}")
+            scales = keep.tile([P, Q], U8, align_bytes=64, name=f"w_scales{g}")
+            nc.vector.quantize_mx(out=codes[:].bitcast(FP8X4), scales=scales[:], in_=w_t[g][:])
+            w_codes.append(codes)
+            w_scales.append(scales)
+
+        out_banks = [psum.tile([P, HALF], F32, name=f"out_bank{h}", tag=f"bank{2 + h}") for h in range(2)]
+        for g in range(passes):
+            for h in range(2):
+                cols = slice(h * HALF, (h + 1) * HALF)
+                nc.tensor.matmul_mx(
+                    out=out_banks[h][:],
+                    lhsT=w_codes[g][:].bitcast(FP8X4),
+                    lhsT_scale=w_scales[g][:],
+                    rhs=v_codes[g][:, cols].bitcast(FP8X4),
+                    rhs_scale=v_scales[g][:, cols],
+                    start=(g == 0),
+                    stop=(g == passes - 1),
+                )
+        left = keep.tile([P, HALF], F32)
+        nc.scalar.copy(out=left[:], in_=out_banks[0][:])
+        nc.scalar.dma_start(out=out[:, :HALF], in_=left[:])
+        right = keep.tile([P, HALF], F32)
+        nc.vector.tensor_copy(out=right[:], in_=out_banks[1][:])
+        nc.sync.dma_start(out=out[:, HALF:], in_=right[:])

@@ -37,38 +37,35 @@ def tile_attend_ownlists_positions_kernel(
         psum = ctx.enter_context(tc.psum_pool(name="psum", bufs=1))
 
         k_scales = keep.tile([P, T], U8, align_bytes=64)
-        warm = keep.tile([P, 1], F32)
-        nc.vector.memset(warm[:], 0.0)
-        warm_out = keep.tile([P, 1], F32)
-        nc.scalar.activation(warm_out[:], warm[:], ACT.Exp)
 
         q_raw = keep.tile([P, PACK, Q], F32)
         nc.sync.dma_start(out=q_raw[:], in_=query.rearrange("(p j) q -> p j q", j=PACK))
         for quad in range(4):
-            nc.scalar.dma_start(
+            nc.sync.dma_start(
                 out=k_scales[32 * quad : 32 * quad + 4, :].bitcast(I32),
                 in_=keys_scales[0, 4 * quad : 4 * quad + 4, :].bitcast(I32),
             )
+        k_words = keep.tile([P, 2 * T], U8, align_bytes=64, tag="v_codes0")
+        nc.sync.dma_start(out=k_words[:].bitcast(I32), in_=keys_words[0].bitcast(I32))
         offsets = keep.tile([P, I // 16], U16)
         nc.sync.dma_start(offsets[:], offs)
         pos_all = keep.tile([P, T], F32)
         nc.sync.dma_start(out=pos_all[:], in_=pos)
-        k_words = keep.tile([P, 2 * T], U8, align_bytes=64)
-        nc.sync.dma_start(out=k_words[:].bitcast(I32), in_=keys_words[0].bitcast(I32))
         qpos_col = keep.tile([P, 1], F32)
         nc.sync.dma_start(out=qpos_col[:], in_=qpos)
         slope_col = keep.tile([P, 1], F32)
         nc.sync.dma_start(out=slope_col[:], in_=slope)
         fac_cols = keep.tile([P, passes, PACK], F32)
         nc.sync.dma_start(out=fac_cols[:], in_=fac.rearrange("o (g p j) -> p (o g) j", g=passes, j=PACK))
-        v_raw = []
-        for g in range(passes):
-            tile_g = keep.tile([P, PACK, E], F32, name=f"v_raw{g}", tag=f"v_raw{g}", align_bytes=64)
-            nc.sync.dma_start(
-                out=tile_g[:],
-                in_=vals[g * K_PASS : (g + 1) * K_PASS, :].rearrange("(p j) e -> p j e", j=PACK),
+        v_raw = {}
+        for g, c0, c1 in ((0, 0, HALF), (0, HALF, E), (1, 0, E)):
+            v_raw[g, c0] = keep.tile(
+                [P, PACK, c1 - c0], F32, name=f"v_raw{g}_{c0}", tag=f"v_raw{g}_{c0}", align_bytes=64
             )
-            v_raw.append(tile_g)
+            nc.sync.dma_start(
+                out=v_raw[g, c0][:],
+                in_=vals[g * K_PASS : (g + 1) * K_PASS, c0:c1].rearrange("(p j) e -> p j e", j=PACK),
+            )
 
         ident = keep.tile([P, P], F32)
         make_identity(nc, ident[:])
@@ -76,23 +73,17 @@ def tile_attend_ownlists_positions_kernel(
         nc.gpsimd.memset(w_full[:], 0.0)
 
         q_bf = keep.tile([P, Q, PACK], BF16, align_bytes=64)
-        nc.vector.tensor_copy(out=q_bf[:], in_=q_raw[:].rearrange("p j q -> p q j"))
+        q_halves = [slice(0, Q // 2), slice(Q // 2, Q)]
+        for rows in q_halves:
+            nc.vector.tensor_copy(out=q_bf[:, rows, :], in_=q_raw[:, :, rows].rearrange("p j q -> p q j"))
         q_codes = keep.tile([P, Q], U32, align_bytes=64)
         q_scales = keep.tile([P, Q], U8, align_bytes=64)
-        nc.vector.quantize_mx(
-            out=q_codes[:].bitcast(FP8X4), scales=q_scales[:], in_=q_bf[:].rearrange("p q j -> p (q j)")
-        )
-
-        pos_listed = keep.tile([P, I], F32)
-        dist2 = keep.tile([P, I], F32)
-        penalty = keep.tile([P, I], F32)
-        for h in range(2):
-            slots = slice(h * HALF, (h + 1) * HALF)
-            nc.vector.tensor_copy(
-                pos_listed[:, slots], pos_all[:].indirect(offsets[:, h * HALF // 16 : (h + 1) * HALF // 16])
+        for rows in q_halves:
+            nc.vector.quantize_mx(
+                out=q_codes[:, rows].bitcast(FP8X4),
+                scales=q_scales[:, rows],
+                in_=q_bf[:, rows, :].rearrange("p q j -> p (q j)"),
             )
-            nc.scalar.activation(dist2[:, slots], pos_listed[:, slots], ACT.Square, bias=qpos_col[:], scale=-1.0)
-            nc.scalar.activation(penalty[:, slots], dist2[:, slots], ACT.Copy, scale=slope_col[:])
 
         scores = keep.tile([P, T], F32)
         for h in range(T // HALF):
@@ -107,80 +98,99 @@ def tile_attend_ownlists_positions_kernel(
                 start=True,
                 stop=True,
             )
-            if h < T // HALF - 1:
-                nc.vector.tensor_copy(out=scores[:, cols], in_=bank[:])
-            else:
-                nc.scalar.copy(out=scores[:, cols], in_=bank[:])
+            nc.scalar.activation(scores[:, cols], bank[:], ACT.Copy)
+
+        pos_listed = keep.tile([P, I], F32, align_bytes=64, tag="v_bf_a")
+        nc.vector.tensor_copy(pos_listed[:], pos_all[:].indirect(offsets[:]))
+        dist2 = keep.tile([P, I], F32, align_bytes=64, tag="v_codes0")
+        nc.scalar.activation(dist2[:], pos_listed[:], ACT.Square, bias=qpos_col[:], scale=-1.0)
 
         fac_banks = []
         for g in range(passes):
-            fac_bank = psum.tile([P, PACK, P], F32, name=f"fac_bank{g}")
+            fac_bank = psum.tile([P, PACK, P], F32, name=f"fac_bank{g}", tag=f"bank{2 + g}")
             for j in range(PACK):
                 nc.tensor.transpose(fac_bank[:, j, :], fac_cols[:, g, j : j + 1].to_broadcast([P, P]), ident[:])
             fac_banks.append(fac_bank)
 
         v_bf = {}
-        v_codes = [keep.tile([P, E], U32, align_bytes=64, name=f"v_codes{g}") for g in range(passes)]
+        v_codes = {}
         v_scales = [keep.tile([P, E], U8, align_bytes=64, name=f"v_scales{g}") for g in range(passes)]
 
-        def cast_values(g, c0, c1, tag):
-            v_bf[g, c0] = keep.tile([P, c1 - c0, PACK], BF16, align_bytes=64, name=f"v_bf{g}_{c0}", tag=tag)
+        def cast_values(g, c0, dst):
             nc.scalar.copy(
-                out=v_bf[g, c0][:].rearrange("p (c i) j -> p c j i", i=4),
-                in_=v_raw[g][:, :, c0:c1].rearrange("p j (c i) -> p c j i", i=4),
+                out=dst.rearrange("p (c i) j -> p c j i", i=4),
+                in_=v_raw[g, c0][:].rearrange("p j (c i) -> p c j i", i=4),
             )
 
-        def quantise_values(g, c0, c1):
+        def quantise_values(g, c0, c1, tag):
+            codes = keep.tile([P, c1 - c0], U32, align_bytes=64, name=f"v_codes{g}_{c0}", tag=tag)
+            for c in range(c0, c1, HALF):
+                v_codes[g, c // HALF] = codes[:, c - c0 : c - c0 + HALF]
             nc.vector.quantize_mx(
-                out=v_codes[g][:, c0:c1].bitcast(FP8X4),
+                out=codes[:].bitcast(FP8X4),
                 scales=v_scales[g][:, c0:c1],
                 in_=v_bf[g, c0][:].rearrange("p e j -> p (e j)"),
             )
 
         s = keep.tile([P, I], F32, align_bytes=64, tag="shared")
-        nc.vector.tensor_tensor(s[:], scores[:].indirect(offsets[:]), penalty[:], ALU.subtract)
+        scores_listed = keep.tile([P, I], F32)
+        for h in range(2):
+            nc.vector.tensor_copy(
+                scores_listed[:, h * HALF : (h + 1) * HALF],
+                scores[:].indirect(offsets[:, h * HALF // 16 : (h + 1) * HALF // 16]),
+            )
+        for h in range(2):
+            slots = slice(h * HALF, (h + 1) * HALF)
+            nc.vector.scalar_tensor_tensor(
+                out=s[:, slots],
+                in0=dist2[:, slots],
+                scalar=slope_col[:],
+                in1=scores_listed[:, slots],
+                op0=ALU.mult,
+                op1=ALU.subtract,
+            )
         neg_max = keep.tile([P, 1], F32)
-        nc.vector.tensor_reduce(neg_max[:], s[:], AXIS.X, ALU.max, negate=True)
-        cast_values(0, 0, HALF, "v_bf_a")
-        p_head = v_raw[0][:, 0, :HEAD]
-        nc.scalar.activation(p_head, s[:, :HEAD], ACT.Exp, bias=neg_max[:])
-        p_all = keep.tile([P, I], F32)
+        nc.vector.tensor_reduce(neg_max[:], s[:], AXIS.X, ALU.min)
+        v_bf[0, 0] = keep.tile([P, HALF, PACK], BF16, align_bytes=64, name="v_bf00", tag="v_bf_a")
+        cast_values(0, 0, v_bf[0, 0][:])
+        weights = keep.tile([P, I], F32, align_bytes=64, tag="v_raw0_0")
         row_sum = keep.tile([P, 1], F32)
-        nc.scalar.activation(p_all[:], s[:], ACT.Exp, bias=neg_max[:], accum_out=row_sum[:])
-        quantise_values(0, 0, HALF)
-        nc.vector.tensor_copy(w_full[:].indirect(offsets[:, : HEAD // 16]), p_head)
+        nc.scalar.activation(weights[:], s[:], ACT.Exp, bias=neg_max[:], scale=-1.0, accum_out=row_sum[:])
+        quantise_values(0, 0, HALF, "v_codes0")
+        nc.vector.tensor_copy(w_full[:].indirect(offsets[:]), weights[:])
         inv_sum = keep.tile([P, 1], F32)
         nc.vector.reciprocal(inv_sum[:], row_sum[:])
-        nc.vector.tensor_copy(w_full[:].indirect(offsets[:, HEAD // 16 :]), p_all[:, HEAD:])
-        cast_values(0, HALF, E, "shared")
-        cast_values(1, 0, HALF, "v_bf_b")
-        cast_values(1, HALF, E, "v_bf_c")
-        quantise_values(0, HALF, E)
+        v_rest = keep.tile([P, HALF + E, PACK], BF16, align_bytes=64, tag="shared")
+        v_bf[0, HALF] = v_rest[:, :HALF, :]
+        v_bf[1, 0] = v_rest[:, HALF:, :]
+        cast_values(0, HALF, v_bf[0, HALF])
+        cast_values(1, 0, v_bf[1, 0])
+        quantise_values(0, HALF, E, "v_codes0b")
 
         w_t = []
         for g in range(passes):
-            w_bf = keep.tile([P, K_PASS], BF16, align_bytes=64, name=f"w_bf{g}", tag=("shared", "w_bf")[g])
-            nc.vector.scalar_tensor_tensor(
-                out=w_bf[:].rearrange("q (p j) -> q p j", j=PACK),
-                in0=w_full[:, g * K_PASS : (g + 1) * K_PASS].rearrange("q (p j) -> q p j", j=PACK),
-                scalar=inv_sum[:],
-                in1=fac_banks[g][:].rearrange("q j p -> q p j"),
-                op0=ALU.mult,
-                op1=ALU.mult,
-            )
-            pairs = w_bf[:].bitcast(F32)
+            w_bf = keep.tile([P, K_PASS], BF16, align_bytes=64, name=f"w_bf{g}", tag=("v_raw0_256", "w_bf")[g])
             turned = psum.tile([P, 2, Q], F32, name=f"turned{g}", tag=f"bank{g}")
+            w_pass = w_full[:, g * K_PASS : (g + 1) * K_PASS].rearrange("q (p j) -> q p j", j=PACK)
             for u in range(2):
-                nc.tensor.transpose(turned[:, u, :], pairs[:, u : K_PASS // 2 : 2], ident[:])
-            w_tg = keep.tile([P, Q * PACK], BF16, align_bytes=64, name=f"w_t{g}", tag=f"v_raw{1 - g}")
+                pair = w_bf[:, u * HALF : (u + 1) * HALF]
+                nc.vector.scalar_tensor_tensor(
+                    out=pair.rearrange("q (p e) -> q p e", e=2),
+                    in0=w_pass[:, :, 2 * u : 2 * u + 2],
+                    scalar=inv_sum[:],
+                    in1=fac_banks[g][:, 2 * u : 2 * u + 2, :].rearrange("q e p -> q p e"),
+                    op0=ALU.mult,
+                    op1=ALU.mult,
+                )
+                nc.tensor.transpose(turned[:, u, :], pair.bitcast(F32), ident[:])
+            w_tg = keep.tile([P, Q * PACK], BF16, align_bytes=64, name=f"w_t{g}", tag=("v_raw1_0", "w_t1")[g])
             nc.scalar.copy(
                 out=w_tg[:].bitcast(F32).rearrange("p (q u) -> p q u", u=2),
                 in_=turned[:].rearrange("p u q -> p q u"),
             )
             w_t.append(w_tg)
 
-        quantise_values(1, 0, HALF)
-        quantise_values(1, HALF, E)
+        quantise_values(1, 0, E, "v_raw0_256")
 
         w_codes = []
         w_scales = []
@@ -191,22 +201,24 @@ def tile_attend_ownlists_positions_kernel(
             w_codes.append(codes)
             w_scales.append(scales)
 
-        out_banks = [psum.tile([P, HALF], F32, name=f"out_bank{h}", tag=f"bank{2 + h}") for h in range(2)]
+        pieces = ((0, HALF), (HALF, HALF + P), (HALF + P, E))
+        out_banks = [psum.tile([P, c1 - c0], F32, name=f"out_bank{c0}") for c0, c1 in pieces]
         for g in range(passes):
-            for h in range(2):
-                cols = slice(h * HALF, (h + 1) * HALF)
+            for bank, (c0, c1) in zip(out_banks, pieces):
+                h = c0 // HALF
                 nc.tensor.matmul_mx(
-                    out=out_banks[h][:],
+                    out=bank[:],
                     lhsT=w_codes[g][:].bitcast(FP8X4),
                     lhsT_scale=w_scales[g][:],
-                    rhs=v_codes[g][:, cols].bitcast(FP8X4),
-                    rhs_scale=v_scales[g][:, cols],
+                    rhs=v_codes[g, h][:, c0 - h * HALF : c1 - h * HALF].bitcast(FP8X4),
+                    rhs_scale=v_scales[g][:, c0:c1],
                     start=(g == 0),
                     stop=(g == passes - 1),
                 )
-        left = keep.tile([P, HALF], F32)
-        nc.scalar.copy(out=left[:], in_=out_banks[0][:])
-        nc.scalar.dma_start(out=out[:, :HALF], in_=left[:])
-        right = keep.tile([P, HALF], F32)
-        nc.vector.tensor_copy(out=right[:], in_=out_banks[1][:])
-        nc.sync.dma_start(out=out[:, HALF:], in_=right[:])
+        for n, (bank, (c0, c1)) in enumerate(zip(out_banks, pieces)):
+            result = keep.tile([P, c1 - c0], F32, name=f"result{n}")
+            if n == 1:
+                nc.vector.tensor_copy(out=result[:], in_=bank[:])
+            else:
+                nc.scalar.copy(out=result[:], in_=bank[:])
+            (nc.scalar if n == 2 else nc.sync).dma_start(out=out[:, c0:c1], in_=result[:])

@@ -160,16 +160,15 @@ def tile_attend_ownlists_positions_kernel(
         nc.vector.tensor_copy(w_full[:].indirect(offsets[:]), weights[:])
         inv_sum = keep.tile([P, 1], F32)
         nc.vector.reciprocal(inv_sum[:], row_sum[:])
-        v_rest = keep.tile([P, HALF + E, PACK], BF16, align_bytes=64, tag="shared")
-        v_bf[0, HALF] = v_rest[:, :HALF, :]
-        v_bf[1, 0] = v_rest[:, HALF:, :]
-        cast_values(0, HALF, v_bf[0, HALF])
-        cast_values(1, 0, v_bf[1, 0])
+        v_bf[0, HALF] = keep.tile([P, HALF, PACK], BF16, align_bytes=64, name="v_bf01", tag="shared")
+        cast_values(0, HALF, v_bf[0, HALF][:])
+        v_bf[1, 0] = keep.tile([P, E, PACK], BF16, align_bytes=64, name="v_bf1", tag="v_raw0_256")
+        cast_values(1, 0, v_bf[1, 0][:])
         quantise_values(0, HALF, E, "v_codes0b")
 
         w_t = []
         for g in range(passes):
-            w_bf = keep.tile([P, K_PASS], BF16, align_bytes=64, name=f"w_bf{g}", tag=("v_raw0_256", "w_bf")[g])
+            w_bf = keep.tile([P, K_PASS], BF16, align_bytes=64, name=f"w_bf{g}", tag=f"w_bf{g}")
             turned = psum.tile([P, 2, Q], F32, name=f"turned{g}", tag=f"bank{g}")
             w_pass = w_full[:, g * K_PASS : (g + 1) * K_PASS].rearrange("q (p j) -> q p j", j=PACK)
             for u in range(2):
@@ -190,7 +189,7 @@ def tile_attend_ownlists_positions_kernel(
             )
             w_t.append(w_tg)
 
-        quantise_values(1, 0, E, "v_raw0_256")
+        quantise_values(1, 0, E, "w_bf0")
 
         w_codes = []
         w_scales = []

@@ -24,6 +24,8 @@ K_PASS = P * PACK
 BANK = 512
 HALF = 256
 HEAD = 128
+LAST = E - 128
+UNLISTED = 2.0**100
 
 
 def tile_attend_ownlists_positions_kernel(
@@ -38,6 +40,8 @@ def tile_attend_ownlists_positions_kernel(
 
         k_scales = keep.tile([P, T], U8, align_bytes=64)
 
+        pos_cols = keep.tile([P, PACK], F32, align_bytes=64, tag="q_codes")
+        nc.sync.dma_start(out=pos_cols[:], in_=pos[0:1, K_PASS:].rearrange("o (p j) -> p (o j)", j=PACK))
         q_raw = keep.tile([P, PACK, Q], F32)
         nc.sync.dma_start(out=q_raw[:], in_=query.rearrange("(p j) q -> p j q", j=PACK))
         for quad in range(4):
@@ -47,10 +51,10 @@ def tile_attend_ownlists_positions_kernel(
             )
         k_words = keep.tile([P, 2 * T], U8, align_bytes=64, tag="v_codes0")
         nc.sync.dma_start(out=k_words[:].bitcast(I32), in_=keys_words[0].bitcast(I32))
+        pos_all = keep.tile([P, T], F32)
+        nc.sync.dma_start(out=pos_all[:, :K_PASS], in_=pos[:, :K_PASS])
         offsets = keep.tile([P, I // 16], U16)
         nc.sync.dma_start(offsets[:], offs)
-        pos_all = keep.tile([P, T], F32)
-        nc.sync.dma_start(out=pos_all[:], in_=pos)
         qpos_col = keep.tile([P, 1], F32)
         nc.sync.dma_start(out=qpos_col[:], in_=qpos)
         slope_col = keep.tile([P, 1], F32)
@@ -58,7 +62,7 @@ def tile_attend_ownlists_positions_kernel(
         fac_cols = keep.tile([P, passes, PACK], F32)
         nc.sync.dma_start(out=fac_cols[:], in_=fac.rearrange("o (g p j) -> p (o g) j", g=passes, j=PACK))
         v_raw = {}
-        for g, c0, c1 in ((0, 0, HALF), (0, HALF, E), (1, 0, E)):
+        for g, c0, c1 in ((0, 0, HALF), (0, HALF, E), (1, 0, P), (1, P, LAST), (1, LAST, E)):
             v_raw[g, c0] = keep.tile(
                 [P, PACK, c1 - c0], F32, name=f"v_raw{g}_{c0}", tag=f"v_raw{g}_{c0}", align_bytes=64
             )
@@ -69,8 +73,15 @@ def tile_attend_ownlists_positions_kernel(
 
         ident = keep.tile([P, P], F32)
         make_identity(nc, ident[:])
-        w_full = keep.tile([P, T], F32)
-        nc.gpsimd.memset(w_full[:], 0.0)
+        w_full = keep.tile([P, T], F32, align_bytes=64)
+        nc.vector.memset(w_full[:], UNLISTED)
+
+        pos_bank = psum.tile([P, PACK, P], F32)
+        for j in range(PACK):
+            nc.tensor.transpose(pos_bank[:, j, :], pos_cols[:, j : j + 1].to_broadcast([P, P]), ident[:])
+        nc.scalar.activation(
+            pos_all[:, K_PASS:].rearrange("q (p j) -> q p j", j=PACK), pos_bank[:].rearrange("q j p -> q p j"), ACT.Copy
+        )
 
         q_bf = keep.tile([P, Q, PACK], BF16, align_bytes=64)
         q_halves = [slice(0, Q // 2), slice(Q // 2, Q)]
@@ -101,9 +112,13 @@ def tile_attend_ownlists_positions_kernel(
             nc.scalar.activation(scores[:, cols], bank[:], ACT.Copy)
 
         pos_listed = keep.tile([P, I], F32, align_bytes=64, tag="v_bf_a")
-        nc.vector.tensor_copy(pos_listed[:], pos_all[:].indirect(offsets[:]))
         dist2 = keep.tile([P, I], F32, align_bytes=64, tag="v_codes0")
-        nc.scalar.activation(dist2[:], pos_listed[:], ACT.Square, bias=qpos_col[:], scale=-1.0)
+        for h in range(2):
+            slots = slice(h * HALF, (h + 1) * HALF)
+            nc.vector.tensor_copy(
+                pos_listed[:, slots], pos_all[:].indirect(offsets[:, h * HALF // 16 : (h + 1) * HALF // 16])
+            )
+            nc.scalar.activation(dist2[:, slots], pos_listed[:, slots], ACT.Square, bias=qpos_col[:], scale=-1.0)
 
         fac_banks = []
         for g in range(passes):
@@ -120,16 +135,6 @@ def tile_attend_ownlists_positions_kernel(
             nc.scalar.copy(
                 out=dst.rearrange("p (c i) j -> p c j i", i=4),
                 in_=v_raw[g, c0][:].rearrange("p j (c i) -> p c j i", i=4),
-            )
-
-        def quantise_values(g, c0, c1, tag):
-            codes = keep.tile([P, c1 - c0], U32, align_bytes=64, name=f"v_codes{g}_{c0}", tag=tag)
-            for c in range(c0, c1, HALF):
-                v_codes[g, c // HALF] = codes[:, c - c0 : c - c0 + HALF]
-            nc.vector.quantize_mx(
-                out=codes[:].bitcast(FP8X4),
-                scales=v_scales[g][:, c0:c1],
-                in_=v_bf[g, c0][:].rearrange("p e j -> p (e j)"),
             )
 
         s = keep.tile([P, I], F32, align_bytes=64, tag="shared")
@@ -149,23 +154,33 @@ def tile_attend_ownlists_positions_kernel(
                 op0=ALU.mult,
                 op1=ALU.subtract,
             )
+        nc.vector.tensor_copy(w_full[:].indirect(offsets[:, : HEAD // 16]), s[:, :HEAD])
         neg_max = keep.tile([P, 1], F32)
         nc.vector.tensor_reduce(neg_max[:], s[:], AXIS.X, ALU.min)
-        v_bf[0, 0] = keep.tile([P, HALF, PACK], BF16, align_bytes=64, name="v_bf00", tag="v_bf_a")
-        cast_values(0, 0, v_bf[0, 0][:])
-        weights = keep.tile([P, I], F32, align_bytes=64, tag="v_raw0_0")
+        nc.vector.tensor_copy(w_full[:].indirect(offsets[:, HEAD // 16 :]), s[:, HEAD:])
+        for g, c0, c1, tag in ((0, 0, HALF, "v_bf_a"), (0, HALF, E, "v_bf01"), (1, 0, P, "v_bf10")):
+            v_bf[g, c0] = keep.tile([P, c1 - c0, PACK], BF16, align_bytes=64, name=f"v_bf{g}_{c0}", tag=tag)
+            cast_values(g, c0, v_bf[g, c0][:])
+        listed_exp = keep.tile([P, I], F32, align_bytes=64, tag="v_raw1_0")
         row_sum = keep.tile([P, 1], F32)
-        nc.scalar.activation(weights[:], s[:], ACT.Exp, bias=neg_max[:], scale=-1.0, accum_out=row_sum[:])
-        quantise_values(0, 0, HALF, "v_codes0")
-        nc.vector.tensor_copy(w_full[:].indirect(offsets[:]), weights[:])
+        nc.scalar.activation(listed_exp[:], s[:], ACT.Exp, bias=neg_max[:], scale=-1.0, accum_out=row_sum[:])
+        v_bf[1, P] = keep.tile([P, LAST - P, PACK], BF16, align_bytes=64, name="v_bf11")
+        cast_values(1, P, v_bf[1, P][:])
         inv_sum = keep.tile([P, 1], F32)
         nc.vector.reciprocal(inv_sum[:], row_sum[:])
-        v_bf[0, HALF] = keep.tile([P, HALF, PACK], BF16, align_bytes=64, name="v_bf01", tag="shared")
-        cast_values(0, HALF, v_bf[0, HALF][:])
-        v_bf[1, 0] = keep.tile([P, E, PACK], BF16, align_bytes=64, name="v_bf1", tag="v_raw0_256")
-        cast_values(1, 0, v_bf[1, 0][:])
-        quantise_values(0, HALF, E, "v_codes0b")
 
+        def quantise_values(g, tile_c0, c0, c1):
+            nc.vector.quantize_mx(
+                out=v_codes[g][:, c0:c1].bitcast(FP8X4),
+                scales=v_scales[g][:, c0:c1],
+                in_=v_bf[g, tile_c0][:, c0 - tile_c0 : c1 - tile_c0, :].rearrange("p e j -> p (e j)"),
+            )
+
+        v_codes[0] = keep.tile([P, E], U32, align_bytes=64, name="v_codes_pass0", tag="shared")
+        quantise_values(0, 0, 0, HALF)
+        quantise_values(0, HALF, HALF, E)
+
+        p_full = keep.tile([P, passes * 2, HALF], F32, align_bytes=64, tag="v_raw1_128")
         w_t = []
         for g in range(passes):
             w_bf = keep.tile([P, K_PASS], BF16, align_bytes=64, name=f"w_bf{g}", tag=f"w_bf{g}")
@@ -173,43 +188,49 @@ def tile_attend_ownlists_positions_kernel(
             w_pass = w_full[:, g * K_PASS : (g + 1) * K_PASS].rearrange("q (p j) -> q p j", j=PACK)
             for u in range(2):
                 pair = w_bf[:, u * HALF : (u + 1) * HALF]
+                p_pair = p_full[:, 2 * g + u, :].rearrange("q (p e) -> q p e", e=2)
+                nc.scalar.activation(p_pair, w_pass[:, :, 2 * u : 2 * u + 2], ACT.Exp, bias=neg_max[:], scale=-1.0)
                 nc.vector.scalar_tensor_tensor(
                     out=pair.rearrange("q (p e) -> q p e", e=2),
-                    in0=w_pass[:, :, 2 * u : 2 * u + 2],
+                    in0=p_pair,
                     scalar=inv_sum[:],
                     in1=fac_banks[g][:, 2 * u : 2 * u + 2, :].rearrange("q e p -> q p e"),
                     op0=ALU.mult,
                     op1=ALU.mult,
                 )
                 nc.tensor.transpose(turned[:, u, :], pair.bitcast(F32), ident[:])
-            w_tg = keep.tile([P, Q * PACK], BF16, align_bytes=64, name=f"w_t{g}", tag=("v_raw1_0", "w_t1")[g])
-            nc.scalar.copy(
-                out=w_tg[:].bitcast(F32).rearrange("p (q u) -> p q u", u=2),
-                in_=turned[:].rearrange("p u q -> p q u"),
-            )
-            w_t.append(w_tg)
-
-        quantise_values(1, 0, E, "w_bf0")
+            w_t.append((turned, keep.tile([P, Q * PACK], BF16, align_bytes=64, name=f"w_t{g}")))
 
         w_codes = []
         w_scales = []
         for g in range(passes):
+            turned, w_tg = w_t[g]
+            nc.scalar.copy(
+                out=w_tg[:].bitcast(F32).rearrange("p (q u) -> p q u", u=2),
+                in_=turned[:].rearrange("p u q -> p q u"),
+            )
             codes = keep.tile([P, Q], U32, align_bytes=64, name=f"w_codes{g}")
             scales = keep.tile([P, Q], U8, align_bytes=64, name=f"w_scales{g}")
-            nc.vector.quantize_mx(out=codes[:].bitcast(FP8X4), scales=scales[:], in_=w_t[g][:])
+            nc.vector.quantize_mx(out=codes[:].bitcast(FP8X4), scales=scales[:], in_=w_tg[:])
             w_codes.append(codes)
             w_scales.append(scales)
+            if g == 0:
+                v_bf[1, LAST] = keep.tile([P, E - LAST, PACK], BF16, align_bytes=64, name="v_bf_last", tag="w_full")
+                cast_values(1, LAST, v_bf[1, LAST][:])
+                v_codes[1] = keep.tile([P, E], U32, align_bytes=64, name="v_codes_pass1", tag="v_raw1_128")
+                quantise_values(1, 0, 0, P)
+                quantise_values(1, P, P, LAST)
+                quantise_values(1, LAST, LAST, E)
 
         pieces = ((0, HALF), (HALF, HALF + P), (HALF + P, E))
         out_banks = [psum.tile([P, c1 - c0], F32, name=f"out_bank{c0}") for c0, c1 in pieces]
         for g in range(passes):
             for bank, (c0, c1) in zip(out_banks, pieces):
-                h = c0 // HALF
                 nc.tensor.matmul_mx(
                     out=bank[:],
                     lhsT=w_codes[g][:].bitcast(FP8X4),
                     lhsT_scale=w_scales[g][:],
-                    rhs=v_codes[g, h][:, c0 - h * HALF : c1 - h * HALF].bitcast(FP8X4),
+                    rhs=v_codes[g][:, c0:c1].bitcast(FP8X4),
                     rhs_scale=v_scales[g][:, c0:c1],
                     start=(g == 0),
                     stop=(g == passes - 1),

@@ -25,6 +25,7 @@ BANK = 512
 HALF = 256
 HEAD = 128
 LAST = E - 128
+LATE = E - 64
 UNLISTED = 2.0**100
 
 
@@ -62,7 +63,7 @@ def tile_attend_ownlists_positions_kernel(
         fac_cols = keep.tile([P, passes, PACK], F32)
         nc.sync.dma_start(out=fac_cols[:], in_=fac.rearrange("o (g p j) -> p (o g) j", g=passes, j=PACK))
         v_raw = {}
-        for g, c0, c1 in ((0, 0, HALF), (0, HALF, E), (1, 0, P), (1, P, LAST), (1, LAST, E)):
+        for g, c0, c1 in ((0, 0, HALF), (0, HALF, E), (1, HALF, LAST), (1, 0, HALF), (1, LAST, E)):
             v_raw[g, c0] = keep.tile(
                 [P, PACK, c1 - c0], F32, name=f"v_raw{g}_{c0}", tag=f"v_raw{g}_{c0}", align_bytes=64
             )
@@ -74,9 +75,9 @@ def tile_attend_ownlists_positions_kernel(
         ident = keep.tile([P, P], F32)
         make_identity(nc, ident[:])
         w_full = keep.tile([P, T], F32, align_bytes=64)
-        nc.vector.memset(w_full[:], UNLISTED)
+        nc.gpsimd.memset(w_full[:], UNLISTED)
 
-        pos_bank = psum.tile([P, PACK, P], F32)
+        pos_bank = psum.tile([P, PACK, P], F32, tag="out_bank0")
         for j in range(PACK):
             nc.tensor.transpose(pos_bank[:, j, :], pos_cols[:, j : j + 1].to_broadcast([P, P]), ident[:])
         nc.scalar.activation(
@@ -111,14 +112,12 @@ def tile_attend_ownlists_positions_kernel(
             )
             nc.scalar.activation(scores[:, cols], bank[:], ACT.Copy)
 
-        pos_listed = keep.tile([P, I], F32, align_bytes=64, tag="v_bf_a")
         dist2 = keep.tile([P, I], F32, align_bytes=64, tag="v_codes0")
         for h in range(2):
             slots = slice(h * HALF, (h + 1) * HALF)
-            nc.vector.tensor_copy(
-                pos_listed[:, slots], pos_all[:].indirect(offsets[:, h * HALF // 16 : (h + 1) * HALF // 16])
-            )
-            nc.scalar.activation(dist2[:, slots], pos_listed[:, slots], ACT.Square, bias=qpos_col[:], scale=-1.0)
+            pos_listed = keep.tile([P, HALF], F32, align_bytes=64, name=f"pos_listed{h}", tag=("v_bf_a", "pos_b")[h])
+            nc.vector.tensor_copy(pos_listed[:], pos_all[:].indirect(offsets[:, h * HALF // 16 : (h + 1) * HALF // 16]))
+            nc.scalar.activation(dist2[:, slots], pos_listed[:], ACT.Square, bias=qpos_col[:], scale=-1.0)
 
         fac_banks = []
         for g in range(passes):
@@ -131,10 +130,10 @@ def tile_attend_ownlists_positions_kernel(
         v_codes = {}
         v_scales = [keep.tile([P, E], U8, align_bytes=64, name=f"v_scales{g}") for g in range(passes)]
 
-        def cast_values(g, c0, dst):
+        def cast_values(g, c0, dst, skip=0):
             nc.scalar.copy(
                 out=dst.rearrange("p (c i) j -> p c j i", i=4),
-                in_=v_raw[g, c0][:].rearrange("p j (c i) -> p c j i", i=4),
+                in_=v_raw[g, c0][:, :, skip : skip + dst.shape[1]].rearrange("p j (c i) -> p c j i", i=4),
             )
 
         s = keep.tile([P, I], F32, align_bytes=64, tag="shared")
@@ -158,29 +157,33 @@ def tile_attend_ownlists_positions_kernel(
         neg_max = keep.tile([P, 1], F32)
         nc.vector.tensor_reduce(neg_max[:], s[:], AXIS.X, ALU.min)
         nc.vector.tensor_copy(w_full[:].indirect(offsets[:, HEAD // 16 :]), s[:, HEAD:])
-        for g, c0, c1, tag in ((0, 0, HALF, "v_bf_a"), (0, HALF, E, "v_bf01"), (1, 0, P, "v_bf10")):
-            v_bf[g, c0] = keep.tile([P, c1 - c0, PACK], BF16, align_bytes=64, name=f"v_bf{g}_{c0}", tag=tag)
-            cast_values(g, c0, v_bf[g, c0][:])
-        listed_exp = keep.tile([P, I], F32, align_bytes=64, tag="v_raw1_0")
+        v_bf_early = keep.tile([P, E + LATE, PACK], BF16, align_bytes=64, tag="v_bf_a")
+        for g, c0, c1 in ((0, 0, HALF), (0, HALF, E), (1, HALF, LAST)):
+            v_bf[g, c0] = v_bf_early[:, g * E + c0 : g * E + c1, :]
+            cast_values(g, c0, v_bf[g, c0])
+        listed_exp = keep.tile([P, I], F32, align_bytes=64, tag="v_raw1_256")
         row_sum = keep.tile([P, 1], F32)
         nc.scalar.activation(listed_exp[:], s[:], ACT.Exp, bias=neg_max[:], scale=-1.0, accum_out=row_sum[:])
-        v_bf[1, P] = keep.tile([P, LAST - P, PACK], BF16, align_bytes=64, name="v_bf11")
-        cast_values(1, P, v_bf[1, P][:])
+        for c0, c1 in ((0, HALF), (LAST, LATE)):
+            v_bf[1, c0] = v_bf_early[:, E + c0 : E + c1, :]
+            cast_values(1, c0, v_bf[1, c0])
         inv_sum = keep.tile([P, 1], F32)
         nc.vector.reciprocal(inv_sum[:], row_sum[:])
 
-        def quantise_values(g, tile_c0, c0, c1):
+        def quantise_values(g, c0, c1):
+            bf_c0 = max(c for gg, c in v_bf if gg == g and c <= c0)
+            codes_c0 = max(c for gg, c in v_codes if gg == g and c <= c0)
             nc.vector.quantize_mx(
-                out=v_codes[g][:, c0:c1].bitcast(FP8X4),
+                out=v_codes[g, codes_c0][:, c0 - codes_c0 : c1 - codes_c0].bitcast(FP8X4),
                 scales=v_scales[g][:, c0:c1],
-                in_=v_bf[g, tile_c0][:, c0 - tile_c0 : c1 - tile_c0, :].rearrange("p e j -> p (e j)"),
+                in_=v_bf[g, bf_c0][:, c0 - bf_c0 : c1 - bf_c0, :].rearrange("p e j -> p (e j)"),
             )
 
-        v_codes[0] = keep.tile([P, E], U32, align_bytes=64, name="v_codes_pass0", tag="shared")
-        quantise_values(0, 0, 0, HALF)
-        quantise_values(0, HALF, HALF, E)
+        v_codes[0, 0] = keep.tile([P, E], U32, align_bytes=64, name="v_codes_pass0", tag="shared")
+        quantise_values(0, 0, HALF)
+        quantise_values(0, HALF, E)
 
-        p_full = keep.tile([P, passes * 2, HALF], F32, align_bytes=64, tag="v_raw1_128")
+        p_full = keep.tile([P, passes * 2, HALF], F32, align_bytes=64, tag="v_raw1_0")
         w_t = []
         for g in range(passes):
             w_bf = keep.tile([P, K_PASS], BF16, align_bytes=64, name=f"w_bf{g}", tag=f"w_bf{g}")
@@ -188,16 +191,20 @@ def tile_attend_ownlists_positions_kernel(
             w_pass = w_full[:, g * K_PASS : (g + 1) * K_PASS].rearrange("q (p j) -> q p j", j=PACK)
             for u in range(2):
                 pair = w_bf[:, u * HALF : (u + 1) * HALF]
-                p_pair = p_full[:, 2 * g + u, :].rearrange("q (p e) -> q p e", e=2)
-                nc.scalar.activation(p_pair, w_pass[:, :, 2 * u : 2 * u + 2], ACT.Exp, bias=neg_max[:], scale=-1.0)
-                nc.vector.scalar_tensor_tensor(
-                    out=pair.rearrange("q (p e) -> q p e", e=2),
-                    in0=p_pair,
-                    scalar=inv_sum[:],
-                    in1=fac_banks[g][:, 2 * u : 2 * u + 2, :].rearrange("q e p -> q p e"),
-                    op0=ALU.mult,
-                    op1=ALU.mult,
-                )
+                cuts = (0, P // 2, P) if (g, u) == (passes - 1, 1) else (0, P)
+                for p0, p1 in zip(cuts, cuts[1:]):
+                    p_pair = p_full[:, 2 * g + u, 2 * p0 : 2 * p1].rearrange("q (p e) -> q p e", e=2)
+                    nc.scalar.activation(
+                        p_pair, w_pass[:, p0:p1, 2 * u : 2 * u + 2], ACT.Exp, bias=neg_max[:], scale=-1.0
+                    )
+                    nc.vector.scalar_tensor_tensor(
+                        out=pair[:, 2 * p0 : 2 * p1].rearrange("q (p e) -> q p e", e=2),
+                        in0=p_pair,
+                        scalar=inv_sum[:],
+                        in1=fac_banks[g][:, 2 * u : 2 * u + 2, p0:p1].rearrange("q e p -> q p e"),
+                        op0=ALU.mult,
+                        op1=ALU.mult,
+                    )
                 nc.tensor.transpose(turned[:, u, :], pair.bitcast(F32), ident[:])
             w_t.append((turned, keep.tile([P, Q * PACK], BF16, align_bytes=64, name=f"w_t{g}")))
 
@@ -215,30 +222,31 @@ def tile_attend_ownlists_positions_kernel(
             w_codes.append(codes)
             w_scales.append(scales)
             if g == 0:
-                v_bf[1, LAST] = keep.tile([P, E - LAST, PACK], BF16, align_bytes=64, name="v_bf_last", tag="w_full")
-                cast_values(1, LAST, v_bf[1, LAST][:])
-                v_codes[1] = keep.tile([P, E], U32, align_bytes=64, name="v_codes_pass1", tag="v_raw1_128")
-                quantise_values(1, 0, 0, P)
-                quantise_values(1, P, P, LAST)
-                quantise_values(1, LAST, LAST, E)
+                v_bf[1, LATE] = keep.tile([P, E - LATE, PACK], BF16, align_bytes=64, name="v_bf_last", tag="w_bf0")
+                cast_values(1, LAST, v_bf[1, LATE][:], LATE - LAST)
+                v_codes[1, HALF] = keep.tile([P, HALF], U32, align_bytes=64, name="v_codes_1b", tag="v_raw1_0")
+                v_codes[1, 0] = keep.tile([P, HALF], U32, align_bytes=64, name="v_codes_1a", tag="w_bf1")
+                for c0, c1 in ((HALF, LAST), (LAST, LATE), (0, HALF), (LATE, E)):
+                    quantise_values(1, c0, c1)
 
-        pieces = ((0, HALF), (HALF, HALF + P), (HALF + P, E))
+        pieces = [(c0, c0 + P) for c0 in range(0, E, P)]
         out_banks = [psum.tile([P, c1 - c0], F32, name=f"out_bank{c0}") for c0, c1 in pieces]
         for g in range(passes):
             for bank, (c0, c1) in zip(out_banks, pieces):
+                codes_c0 = max(c for gg, c in v_codes if gg == g and c <= c0)
                 nc.tensor.matmul_mx(
                     out=bank[:],
                     lhsT=w_codes[g][:].bitcast(FP8X4),
                     lhsT_scale=w_scales[g][:],
-                    rhs=v_codes[g][:, c0:c1].bitcast(FP8X4),
+                    rhs=v_codes[g, codes_c0][:, c0 - codes_c0 : c1 - codes_c0].bitcast(FP8X4),
                     rhs_scale=v_scales[g][:, c0:c1],
                     start=(g == 0),
                     stop=(g == passes - 1),
                 )
+        result = keep.tile([P, E], F32)
         for n, (bank, (c0, c1)) in enumerate(zip(out_banks, pieces)):
-            result = keep.tile([P, c1 - c0], F32, name=f"result{n}")
-            if n == 1:
-                nc.vector.tensor_copy(out=result[:], in_=bank[:])
+            if n % 2 == 0:
+                nc.scalar.copy(out=result[:, c0:c1], in_=bank[:])
             else:
-                nc.scalar.copy(out=result[:], in_=bank[:])
-            (nc.scalar if n == 2 else nc.sync).dma_start(out=out[:, c0:c1], in_=result[:])
+                nc.vector.tensor_copy(out=result[:, c0:c1], in_=bank[:])
+            (nc.scalar, nc.sync, nc.scalar, nc.sync)[n].dma_start(out=out[:, c0:c1], in_=result[:, c0:c1])

@@ -1,7 +1,6 @@
 from contextlib import ExitStack
 
 import concourse.mybir as mybir
-from concourse.masks import make_identity
 
 D, T, Q, I, E = 512, 1024, 128, 512, 512
 FLOPS = 2 * D * T * Q + 2 * T * Q * E
@@ -41,7 +40,7 @@ def tile_attend_ownlists_positions_kernel(
 
         k_scales = keep.tile([P, T], U8, align_bytes=64)
 
-        pos_cols = keep.tile([P, PACK], F32, align_bytes=64, tag="q_codes")
+        pos_cols = keep.tile([P, PACK], F32)
         nc.sync.dma_start(out=pos_cols[:], in_=pos[0:1, K_PASS:].rearrange("o (p j) -> p (o j)", j=PACK))
         q_raw = keep.tile([P, PACK, Q], F32)
         nc.sync.dma_start(out=q_raw[:], in_=query.rearrange("(p j) q -> p j q", j=PACK))
@@ -56,14 +55,9 @@ def tile_attend_ownlists_positions_kernel(
         nc.sync.dma_start(out=pos_all[:, :K_PASS], in_=pos[:, :K_PASS])
         offsets = keep.tile([P, I // 16], U16)
         nc.sync.dma_start(offsets[:], offs)
-        qpos_col = keep.tile([P, 1], F32)
-        nc.sync.dma_start(out=qpos_col[:], in_=qpos)
-        slope_col = keep.tile([P, 1], F32)
-        nc.sync.dma_start(out=slope_col[:], in_=slope)
-        fac_cols = keep.tile([P, passes, PACK], F32)
-        nc.sync.dma_start(out=fac_cols[:], in_=fac.rearrange("o (g p j) -> p (o g) j", g=passes, j=PACK))
         v_raw = {}
-        for g, c0, c1 in ((0, 0, HALF), (0, HALF, E), (1, HALF, LAST), (1, 0, HALF), (1, LAST, E)):
+
+        def load_values(g, c0, c1):
             v_raw[g, c0] = keep.tile(
                 [P, PACK, c1 - c0], F32, name=f"v_raw{g}_{c0}", tag=f"v_raw{g}_{c0}", align_bytes=64
             )
@@ -72,14 +66,37 @@ def tile_attend_ownlists_positions_kernel(
                 in_=vals[g * K_PASS : (g + 1) * K_PASS, c0:c1].rearrange("(p j) e -> p j e", j=PACK),
             )
 
+        qpos_col = keep.tile([P, 1], F32)
+        nc.sync.dma_start(out=qpos_col[:], in_=qpos)
+        load_values(0, 0, HALF)
+        slope_col = keep.tile([P, 1], F32)
+        nc.sync.dma_start(out=slope_col[:], in_=slope)
+        load_values(0, HALF, E)
+        fac_cols = keep.tile([P, passes, PACK], F32)
+        nc.sync.dma_start(out=fac_cols[:], in_=fac.rearrange("o (g p j) -> p (o g) j", g=passes, j=PACK))
+        load_values(1, 0, HALF)
+        load_values(1, HALF, E)
+
+        zeros = keep.tile([P, P], F32, align_bytes=64, tag="w_full")
+        nc.gpsimd.memset(zeros[:], 0.0)
+        ident_first = keep.tile([P, P], F32, align_bytes=64, tag="q_codes")
         ident = keep.tile([P, P], F32)
-        make_identity(nc, ident[:])
+        for tile in (ident_first, ident):
+            nc.gpsimd.affine_select(
+                out=tile[:],
+                in_=zeros[:],
+                compare_op=ALU.not_equal,
+                fill=1.0,
+                base=0,
+                pattern=[[-1, P]],
+                channel_multiplier=1,
+            )
         w_full = keep.tile([P, T], F32, align_bytes=64)
         nc.gpsimd.memset(w_full[:], UNLISTED)
 
         pos_bank = psum.tile([P, PACK, P], F32, tag="out_bank0")
         for j in range(PACK):
-            nc.tensor.transpose(pos_bank[:, j, :], pos_cols[:, j : j + 1].to_broadcast([P, P]), ident[:])
+            nc.tensor.transpose(pos_bank[:, j, :], pos_cols[:, j : j + 1].to_broadcast([P, P]), (ident if j else ident_first)[:])
         nc.scalar.activation(
             pos_all[:, K_PASS:].rearrange("q (p j) -> q p j", j=PACK), pos_bank[:].rearrange("q j p -> q p j"), ACT.Copy
         )
@@ -158,15 +175,14 @@ def tile_attend_ownlists_positions_kernel(
         nc.vector.tensor_reduce(neg_max[:], s[:], AXIS.X, ALU.min)
         nc.vector.tensor_copy(w_full[:].indirect(offsets[:, HEAD // 16 :]), s[:, HEAD:])
         v_bf_early = keep.tile([P, E + LATE, PACK], BF16, align_bytes=64, tag="v_bf_a")
-        for g, c0, c1 in ((0, 0, HALF), (0, HALF, E), (1, HALF, LAST)):
+        for g, c0, c1 in ((0, 0, HALF), (0, HALF, E), (1, 0, HALF)):
             v_bf[g, c0] = v_bf_early[:, g * E + c0 : g * E + c1, :]
             cast_values(g, c0, v_bf[g, c0])
-        listed_exp = keep.tile([P, I], F32, align_bytes=64, tag="v_raw1_256")
+        listed_exp = keep.tile([P, I], F32, align_bytes=64, tag="v_raw0_256")
         row_sum = keep.tile([P, 1], F32)
         nc.scalar.activation(listed_exp[:], s[:], ACT.Exp, bias=neg_max[:], scale=-1.0, accum_out=row_sum[:])
-        for c0, c1 in ((0, HALF), (LAST, LATE)):
-            v_bf[1, c0] = v_bf_early[:, E + c0 : E + c1, :]
-            cast_values(1, c0, v_bf[1, c0])
+        v_bf[1, HALF] = v_bf_early[:, E + HALF :, :]
+        cast_values(1, HALF, v_bf[1, HALF])
         inv_sum = keep.tile([P, 1], F32)
         nc.vector.reciprocal(inv_sum[:], row_sum[:])
 
@@ -183,7 +199,7 @@ def tile_attend_ownlists_positions_kernel(
         quantise_values(0, 0, HALF)
         quantise_values(0, HALF, E)
 
-        p_full = keep.tile([P, passes * 2, HALF], F32, align_bytes=64, tag="v_raw1_0")
+        p_full = keep.tile([P, passes * 2, HALF], F32, align_bytes=64, tag="v_raw0_256")
         w_t = []
         for g in range(passes):
             w_bf = keep.tile([P, K_PASS], BF16, align_bytes=64, name=f"w_bf{g}", tag=f"w_bf{g}")
@@ -223,8 +239,8 @@ def tile_attend_ownlists_positions_kernel(
             w_scales.append(scales)
             if g == 0:
                 v_bf[1, LATE] = keep.tile([P, E - LATE, PACK], BF16, align_bytes=64, name="v_bf_last", tag="w_bf0")
-                cast_values(1, LAST, v_bf[1, LATE][:], LATE - LAST)
-                v_codes[1, HALF] = keep.tile([P, HALF], U32, align_bytes=64, name="v_codes_1b", tag="v_raw1_0")
+                cast_values(1, HALF, v_bf[1, LATE][:], LATE - HALF)
+                v_codes[1, HALF] = keep.tile([P, HALF], U32, align_bytes=64, name="v_codes_1b", tag="v_raw0_256")
                 v_codes[1, 0] = keep.tile([P, HALF], U32, align_bytes=64, name="v_codes_1a", tag="w_bf1")
                 for c0, c1 in ((HALF, LAST), (LAST, LATE), (0, HALF), (LATE, E)):
                     quantise_values(1, c0, c1)

@@ -49,7 +49,7 @@ def tile_attend_ownlists_positions_kernel(
                 out=k_scales[32 * quad : 32 * quad + 4, :].bitcast(I32),
                 in_=keys_scales[0, 4 * quad : 4 * quad + 4, :].bitcast(I32),
             )
-        k_words = keep.tile([P, 2 * T], U8, align_bytes=64, tag="v_codes0")
+        k_words = keep.tile([P, 2 * T], U8, align_bytes=64, tag="shared")
         nc.sync.dma_start(out=k_words[:].bitcast(I32), in_=keys_words[0].bitcast(I32))
         pos_all = keep.tile([P, T], F32)
         nc.sync.dma_start(out=pos_all[:, :K_PASS], in_=pos[:, :K_PASS])
@@ -129,12 +129,14 @@ def tile_attend_ownlists_positions_kernel(
             )
             nc.scalar.activation(scores[:, cols], bank[:], ACT.Copy)
 
-        dist2 = keep.tile([P, I], F32, align_bytes=64, tag="v_codes0")
-        for h in range(2):
-            slots = slice(h * HALF, (h + 1) * HALF)
+        work = keep.tile([P, 2 * I], F32, align_bytes=64, tag="shared")
+        dist2 = (work[:, I : I + HALF], work[:, I + HALF :])
+        for h in (1, 0):
             pos_listed = keep.tile([P, HALF], F32, align_bytes=64, name=f"pos_listed{h}", tag=("v_bf_a", "pos_b")[h])
             nc.vector.tensor_copy(pos_listed[:], pos_all[:].indirect(offsets[:, h * HALF // 16 : (h + 1) * HALF // 16]))
-            nc.scalar.activation(dist2[:, slots], pos_listed[:], ACT.Square, bias=qpos_col[:], scale=-1.0)
+            nc.scalar.activation(dist2[h], pos_listed[:], ACT.Square, bias=qpos_col[:], scale=-1.0)
+        penalty = keep.tile([P, HALF], F32, align_bytes=64, tag="penalty")
+        nc.scalar.activation(penalty[:], dist2[1], ACT.Copy, scale=slope_col[:])
 
         fac_banks = []
         for g in range(passes):
@@ -153,34 +155,38 @@ def tile_attend_ownlists_positions_kernel(
                 in_=v_raw[g, c0][:, :, skip : skip + dst.shape[1]].rearrange("p j (c i) -> p c j i", i=4),
             )
 
-        s = keep.tile([P, I], F32, align_bytes=64, tag="shared")
+        s = work[:, :I]
         scores_listed = keep.tile([P, I], F32)
         for h in range(2):
             nc.vector.tensor_copy(
                 scores_listed[:, h * HALF : (h + 1) * HALF],
                 scores[:].indirect(offsets[:, h * HALF // 16 : (h + 1) * HALF // 16]),
             )
-        for h in range(2):
-            slots = slice(h * HALF, (h + 1) * HALF)
+        for c0 in (0, HEAD):
             nc.vector.scalar_tensor_tensor(
-                out=s[:, slots],
-                in0=dist2[:, slots],
+                out=s[:, c0 : c0 + HEAD],
+                in0=dist2[0][:, c0 : c0 + HEAD],
                 scalar=slope_col[:],
-                in1=scores_listed[:, slots],
+                in1=scores_listed[:, c0 : c0 + HEAD],
                 op0=ALU.mult,
                 op1=ALU.subtract,
             )
+        nc.gpsimd.tensor_tensor(out=s[:, HALF:], in0=penalty[:], in1=scores_listed[:, HALF:], op=ALU.subtract)
         nc.vector.tensor_copy(w_full[:].indirect(offsets[:, : HEAD // 16]), s[:, :HEAD])
         neg_max = keep.tile([P, 1], F32)
-        nc.vector.tensor_reduce(neg_max[:], s[:], AXIS.X, ALU.min)
+        nc.vector.tensor_reduce(neg_max[:], s, AXIS.X, ALU.min)
         nc.vector.tensor_copy(w_full[:].indirect(offsets[:, HEAD // 16 :]), s[:, HEAD:])
         v_bf_early = keep.tile([P, E + LATE, PACK], BF16, align_bytes=64, tag="v_bf_a")
-        for g, c0, c1 in ((0, 0, HALF), (0, HALF, E), (1, 0, HALF)):
-            v_bf[g, c0] = v_bf_early[:, g * E + c0 : g * E + c1, :]
-            cast_values(g, c0, v_bf[g, c0])
+        v_bf[0, 0] = keep.tile([P, HEAD, PACK], BF16, align_bytes=64, name="v_bf_first", tag="penalty")
+        nc.gpsimd.tensor_copy(out=v_bf[0, 0][:], in_=v_raw[0, 0][:, :, :HEAD].rearrange("p j e -> p e j"))
+        v_bf[0, HEAD] = v_bf_early[:, HEAD:E, :]
+        cast_values(0, 0, v_bf_early[:, HEAD:HALF, :], HEAD)
+        cast_values(0, HALF, v_bf_early[:, HALF:E, :])
+        v_bf[1, 0] = v_bf_early[:, E : E + HALF, :]
+        cast_values(1, 0, v_bf[1, 0])
         listed_exp = keep.tile([P, I], F32, align_bytes=64, tag="v_raw0_256")
         row_sum = keep.tile([P, 1], F32)
-        nc.scalar.activation(listed_exp[:], s[:], ACT.Exp, bias=neg_max[:], scale=-1.0, accum_out=row_sum[:])
+        nc.scalar.activation(listed_exp[:], s, ACT.Exp, bias=neg_max[:], scale=-1.0, accum_out=row_sum[:])
         v_bf[1, HALF] = v_bf_early[:, E + HALF :, :]
         cast_values(1, HALF, v_bf[1, HALF])
         inv_sum = keep.tile([P, 1], F32)
@@ -196,8 +202,9 @@ def tile_attend_ownlists_positions_kernel(
             )
 
         v_codes[0, 0] = keep.tile([P, E], U32, align_bytes=64, name="v_codes_pass0", tag="shared")
-        quantise_values(0, 0, HALF)
         quantise_values(0, HALF, E)
+        quantise_values(0, HEAD, HALF)
+        quantise_values(0, 0, HEAD)
 
         p_full = keep.tile([P, passes * 2, HALF], F32, align_bytes=64, tag="v_raw0_256")
         w_t = []

@@ -23,6 +23,7 @@ K_PASS = P * PACK
 BANK = 512
 HALF = 256
 HEAD = 128
+FIRST = 192
 LAST = E - 128
 LATE = E - 64
 UNLISTED = 2.0**100
@@ -68,9 +69,9 @@ def tile_attend_ownlists_positions_kernel(
 
         qpos_col = keep.tile([P, 1], F32)
         nc.sync.dma_start(out=qpos_col[:], in_=qpos)
-        load_values(0, 0, HALF)
         slope_col = keep.tile([P, 1], F32)
         nc.sync.dma_start(out=slope_col[:], in_=slope)
+        load_values(0, 0, HALF)
         load_values(0, HALF, E)
         fac_cols = keep.tile([P, passes, PACK], F32)
         nc.sync.dma_start(out=fac_cols[:], in_=fac.rearrange("o (g p j) -> p (o g) j", g=passes, j=PACK))
@@ -129,8 +130,8 @@ def tile_attend_ownlists_positions_kernel(
             )
             nc.scalar.activation(scores[:, cols], bank[:], ACT.Copy)
 
-        work = keep.tile([P, 2 * I], F32, align_bytes=64, tag="shared")
-        dist2 = (work[:, I : I + HALF], work[:, I + HALF :])
+        work = keep.tile([P, I + HALF], F32, align_bytes=64, tag="shared")
+        dist2 = (work[:, HALF:I], work[:, I:])
         for h in (1, 0):
             pos_listed = keep.tile([P, HALF], F32, align_bytes=64, name=f"pos_listed{h}", tag=("v_bf_a", "pos_b")[h])
             nc.vector.tensor_copy(pos_listed[:], pos_all[:].indirect(offsets[:, h * HALF // 16 : (h + 1) * HALF // 16]))
@@ -162,20 +163,20 @@ def tile_attend_ownlists_positions_kernel(
                 scores_listed[:, h * HALF : (h + 1) * HALF],
                 scores[:].indirect(offsets[:, h * HALF // 16 : (h + 1) * HALF // 16]),
             )
-        for c0 in (0, HEAD):
+        for c0, c1 in ((0, FIRST), (FIRST, HALF)):
             nc.vector.scalar_tensor_tensor(
-                out=s[:, c0 : c0 + HEAD],
-                in0=dist2[0][:, c0 : c0 + HEAD],
+                out=s[:, c0:c1],
+                in0=dist2[0][:, c0:c1],
                 scalar=slope_col[:],
-                in1=scores_listed[:, c0 : c0 + HEAD],
+                in1=scores_listed[:, c0:c1],
                 op0=ALU.mult,
                 op1=ALU.subtract,
             )
         nc.gpsimd.tensor_tensor(out=s[:, HALF:], in0=penalty[:], in1=scores_listed[:, HALF:], op=ALU.subtract)
-        nc.vector.tensor_copy(w_full[:].indirect(offsets[:, : HEAD // 16]), s[:, :HEAD])
+        nc.vector.tensor_copy(w_full[:].indirect(offsets[:, : FIRST // 16]), s[:, :FIRST])
         neg_max = keep.tile([P, 1], F32)
         nc.vector.tensor_reduce(neg_max[:], s, AXIS.X, ALU.min)
-        nc.vector.tensor_copy(w_full[:].indirect(offsets[:, HEAD // 16 :]), s[:, HEAD:])
+        nc.vector.tensor_copy(w_full[:].indirect(offsets[:, FIRST // 16 :]), s[:, FIRST:])
         v_bf_early = keep.tile([P, E + LATE, PACK], BF16, align_bytes=64, tag="v_bf_a")
         v_bf[0, 0] = keep.tile([P, HEAD, PACK], BF16, align_bytes=64, name="v_bf_first", tag="penalty")
         nc.gpsimd.tensor_copy(out=v_bf[0, 0][:], in_=v_raw[0, 0][:, :, :HEAD].rearrange("p j e -> p e j"))
@@ -201,22 +202,24 @@ def tile_attend_ownlists_positions_kernel(
                 in_=v_bf[g, bf_c0][:, c0 - bf_c0 : c1 - bf_c0, :].rearrange("p e j -> p (e j)"),
             )
 
-        v_codes[0, 0] = keep.tile([P, E], U32, align_bytes=64, name="v_codes_pass0", tag="shared")
-        quantise_values(0, HALF, E)
-        quantise_values(0, HEAD, HALF)
-        quantise_values(0, 0, HEAD)
+        v_codes[0, 0] = keep.tile([P, E], U32, align_bytes=64, name="v_codes_0", tag="v_raw0_256")
+        for c0, c1 in ((HALF, E), (HEAD, HALF), (0, HEAD)):
+            quantise_values(0, c0, c1)
 
-        p_full = keep.tile([P, passes * 2, HALF], F32, align_bytes=64, tag="v_raw0_256")
+        p_early = keep.tile([P, 3, HALF], F32, align_bytes=64)
+        p_last = keep.tile([P, HALF], F32, align_bytes=64, tag="shared")
         w_t = []
         for g in range(passes):
-            w_bf = keep.tile([P, K_PASS], BF16, align_bytes=64, name=f"w_bf{g}", tag=f"w_bf{g}")
+            w_bf = keep.tile([P, K_PASS], BF16, align_bytes=64, name=f"w_bf{g}")
             turned = psum.tile([P, 2, Q], F32, name=f"turned{g}", tag=f"bank{g}")
             w_pass = w_full[:, g * K_PASS : (g + 1) * K_PASS].rearrange("q (p j) -> q p j", j=PACK)
             for u in range(2):
                 pair = w_bf[:, u * HALF : (u + 1) * HALF]
-                cuts = (0, P // 2, P) if (g, u) == (passes - 1, 1) else (0, P)
+                last = (g, u) == (passes - 1, 1)
+                cuts = (0, 3 * P // 4, P) if u else (0, P)
+                p_piece = p_last[:] if last else p_early[:, 2 * g + u, :]
                 for p0, p1 in zip(cuts, cuts[1:]):
-                    p_pair = p_full[:, 2 * g + u, 2 * p0 : 2 * p1].rearrange("q (p e) -> q p e", e=2)
+                    p_pair = p_piece[:, 2 * p0 : 2 * p1].rearrange("q (p e) -> q p e", e=2)
                     nc.scalar.activation(
                         p_pair, w_pass[:, p0:p1, 2 * u : 2 * u + 2], ACT.Exp, bias=neg_max[:], scale=-1.0
                     )
@@ -231,26 +234,33 @@ def tile_attend_ownlists_positions_kernel(
                 nc.tensor.transpose(turned[:, u, :], pair.bitcast(F32), ident[:])
             w_t.append((turned, keep.tile([P, Q * PACK], BF16, align_bytes=64, name=f"w_t{g}")))
 
+        v_codes[1, 0] = keep.tile([P, E], U32, align_bytes=64, name="v_codes_1", tag="p_early")
+        for c0, c1 in ((0, HALF), (HALF, LAST), (LAST, LATE)):
+            quantise_values(1, c0, c1)
+
         w_codes = []
         w_scales = []
         for g in range(passes):
             turned, w_tg = w_t[g]
-            nc.scalar.copy(
-                out=w_tg[:].bitcast(F32).rearrange("p (q u) -> p q u", u=2),
-                in_=turned[:].rearrange("p u q -> p q u"),
-            )
+            for rows in q_halves:
+                nc.scalar.copy(
+                    out=w_tg[:].bitcast(F32).rearrange("p (q u) -> p q u", u=2)[:, rows, :],
+                    in_=turned[:, :, rows].rearrange("p u q -> p q u"),
+                )
             codes = keep.tile([P, Q], U32, align_bytes=64, name=f"w_codes{g}")
             scales = keep.tile([P, Q], U8, align_bytes=64, name=f"w_scales{g}")
-            nc.vector.quantize_mx(out=codes[:].bitcast(FP8X4), scales=scales[:], in_=w_tg[:])
+            for rows in q_halves:
+                nc.vector.quantize_mx(
+                    out=codes[:, rows].bitcast(FP8X4),
+                    scales=scales[:, rows],
+                    in_=w_tg[:, rows.start * PACK : rows.stop * PACK],
+                )
             w_codes.append(codes)
             w_scales.append(scales)
             if g == 0:
                 v_bf[1, LATE] = keep.tile([P, E - LATE, PACK], BF16, align_bytes=64, name="v_bf_last", tag="w_bf0")
                 cast_values(1, HALF, v_bf[1, LATE][:], LATE - HALF)
-                v_codes[1, HALF] = keep.tile([P, HALF], U32, align_bytes=64, name="v_codes_1b", tag="v_raw0_256")
-                v_codes[1, 0] = keep.tile([P, HALF], U32, align_bytes=64, name="v_codes_1a", tag="w_bf1")
-                for c0, c1 in ((HALF, LAST), (LAST, LATE), (0, HALF), (LATE, E)):
-                    quantise_values(1, c0, c1)
+        quantise_values(1, LATE, E)
 
         pieces = [(c0, c0 + P) for c0 in range(0, E, P)]
         out_banks = [psum.tile([P, c1 - c0], F32, name=f"out_bank{c0}") for c0, c1 in pieces]

@@ -20,12 +20,8 @@ AXIS = mybir.AxisListType
 P = 128
 PACK = 4
 K_PASS = P * PACK
-BANK = 512
 HALF = 256
-HEAD = 128
 FIRST = 192
-LAST = E - 128
-LATE = E - 64
 UNLISTED = 2.0**100
 
 
@@ -37,51 +33,61 @@ def tile_attend_ownlists_positions_kernel(
 
     with ExitStack() as ctx:
         keep = ctx.enter_context(tc.tile_pool(name="keep", bufs=1))
+        laid = ctx.enter_context(tc.tile_pool(name="laid", bufs=1))
         psum = ctx.enter_context(tc.psum_pool(name="psum", bufs=1))
 
-        k_scales = keep.tile([P, T], U8, align_bytes=64)
+        def sb(name, shape, dtype, tag=None):
+            return keep.tile(shape, dtype, name=name, tag=tag or name, align_bytes=64)
 
-        pos_cols = keep.tile([P, PACK], F32)
+        def at(offset, name, shape, dtype):
+            return laid.tile(shape, dtype, name=name, tag=name, align_bytes=64, offset=offset)
+
+        pos_cols = sb("pos_cols", [P, PACK], F32)
         nc.sync.dma_start(out=pos_cols[:], in_=pos[0:1, K_PASS:].rearrange("o (p j) -> p (o j)", j=PACK))
-        q_raw = keep.tile([P, PACK, Q], F32)
+        q_raw = sb("q_raw", [P, PACK, Q], F32)
         nc.sync.dma_start(out=q_raw[:], in_=query.rearrange("(p j) q -> p j q", j=PACK))
+        k_scales = sb("k_scales", [P, T], U8)
         for quad in range(4):
             nc.sync.dma_start(
                 out=k_scales[32 * quad : 32 * quad + 4, :].bitcast(I32),
                 in_=keys_scales[0, 4 * quad : 4 * quad + 4, :].bitcast(I32),
             )
-        k_words = keep.tile([P, 2 * T], U8, align_bytes=64, tag="shared")
+        k_words = sb("k_words", [P, 2 * T], U8, tag="costs")
         nc.sync.dma_start(out=k_words[:].bitcast(I32), in_=keys_words[0].bitcast(I32))
-        pos_all = keep.tile([P, T], F32)
+        pos_all = sb("pos_all", [P, T], F32)
         nc.sync.dma_start(out=pos_all[:, :K_PASS], in_=pos[:, :K_PASS])
         offsets = keep.tile([P, I // 16], U16)
         nc.sync.dma_start(offsets[:], offs)
         v_raw = {}
 
-        def load_values(g, c0, c1):
-            v_raw[g, c0] = keep.tile(
-                [P, PACK, c1 - c0], F32, name=f"v_raw{g}_{c0}", tag=f"v_raw{g}_{c0}", align_bytes=64
-            )
+        def load_values(g, c0):
+            if (g, c0) == (0, HALF):
+                v_raw[g, c0] = at(0, f"v_raw{g}_{c0}", [P, PACK, HALF], F32)
+            else:
+                v_raw[g, c0] = sb(f"v_raw{g}_{c0}", [P, PACK, HALF], F32)
             nc.sync.dma_start(
                 out=v_raw[g, c0][:],
-                in_=vals[g * K_PASS : (g + 1) * K_PASS, c0:c1].rearrange("(p j) e -> p j e", j=PACK),
+                in_=vals[g * K_PASS : (g + 1) * K_PASS, c0 : c0 + HALF].rearrange("(p j) e -> p j e", j=PACK),
             )
 
-        qpos_col = keep.tile([P, 1], F32)
+        qpos_col = sb("qpos_col", [P, 1], F32)
         nc.sync.dma_start(out=qpos_col[:], in_=qpos)
-        slope_col = keep.tile([P, 1], F32)
+        slope_col = sb("slope_col", [P, 1], F32)
         nc.sync.dma_start(out=slope_col[:], in_=slope)
-        load_values(0, 0, HALF)
-        load_values(0, HALF, E)
-        fac_cols = keep.tile([P, passes, PACK], F32)
+        load_values(0, 0)
+        load_values(0, HALF)
+        fac_cols = sb("fac_cols", [P, passes, PACK], F32)
         nc.sync.dma_start(out=fac_cols[:], in_=fac.rearrange("o (g p j) -> p (o g) j", g=passes, j=PACK))
-        load_values(1, 0, HALF)
-        load_values(1, HALF, E)
+        load_values(1, 0)
+        load_values(1, HALF)
 
-        zeros = keep.tile([P, P], F32, align_bytes=64, tag="w_full")
+        def listed(window, half):
+            return window[:].indirect(offsets[:, half * HALF // 16 : (half + 1) * HALF // 16])
+
+        zeros = sb("zeros", [P, P], F32, tag="w_full")
         nc.gpsimd.memset(zeros[:], 0.0)
-        ident_first = keep.tile([P, P], F32, align_bytes=64, tag="q_codes")
-        ident = keep.tile([P, P], F32)
+        ident_first = sb("ident_first", [P, P], F32, tag="q_codes")
+        ident = sb("ident", [P, P], F32)
         for tile in (ident_first, ident):
             nc.gpsimd.affine_select(
                 out=tile[:],
@@ -92,22 +98,30 @@ def tile_attend_ownlists_positions_kernel(
                 pattern=[[-1, P]],
                 channel_multiplier=1,
             )
-        w_full = keep.tile([P, T], F32, align_bytes=64)
+        w_full = sb("w_full", [P, T], F32)
         nc.gpsimd.memset(w_full[:], UNLISTED)
+
+        minus_ones = sb("minus_ones", [P, P], F32)
+        nc.gpsimd.memset(minus_ones[:], -1.0)
 
         pos_bank = psum.tile([P, PACK, P], F32, tag="out_bank0")
         for j in range(PACK):
-            nc.tensor.transpose(pos_bank[:, j, :], pos_cols[:, j : j + 1].to_broadcast([P, P]), (ident if j else ident_first)[:])
+            nc.tensor.transpose(
+                pos_bank[:, j, :], pos_cols[:, j : j + 1].to_broadcast([P, P]), (ident if j else ident_first)[:]
+            )
         nc.scalar.activation(
             pos_all[:, K_PASS:].rearrange("q (p j) -> q p j", j=PACK), pos_bank[:].rearrange("q j p -> q p j"), ACT.Copy
         )
 
-        q_bf = keep.tile([P, Q, PACK], BF16, align_bytes=64)
+        q_bf = sb("q_bf", [P, Q, PACK], BF16)
         q_halves = [slice(0, Q // 2), slice(Q // 2, Q)]
-        for rows in q_halves:
-            nc.vector.tensor_copy(out=q_bf[:, rows, :], in_=q_raw[:, :, rows].rearrange("p j q -> p q j"))
-        q_codes = keep.tile([P, Q], U32, align_bytes=64)
-        q_scales = keep.tile([P, Q], U8, align_bytes=64)
+        nc.vector.tensor_copy(out=q_bf[:, :64, :], in_=q_raw[:, :, :64].rearrange("p j q -> p q j"))
+        nc.scalar.copy(
+            out=q_bf[:, 64:, :].rearrange("p (c i) j -> p c j i", i=4),
+            in_=q_raw[:, :, 64:].rearrange("p j (c i) -> p c j i", i=4),
+        )
+        q_codes = sb("q_codes", [P, Q], U32)
+        q_scales = sb("q_scales", [P, Q], U8)
         for rows in q_halves:
             nc.vector.quantize_mx(
                 out=q_codes[:, rows].bitcast(FP8X4),
@@ -115,29 +129,39 @@ def tile_attend_ownlists_positions_kernel(
                 in_=q_bf[:, rows, :].rearrange("p q j -> p (q j)"),
             )
 
-        scores = keep.tile([P, T], F32)
-        for h in range(T // HALF):
-            cols = slice(h * HALF, (h + 1) * HALF)
-            bank = psum.tile([P, HALF], F32, name=f"score_bank{h}", tag=f"bank{h}")
+        scores = sb("scores", [P, T], F32)
+        cuts = (0, 128, 384, 640, 896, T)
+        for h, (t0, t1) in enumerate(zip(cuts, cuts[1:])):
+            cols = slice(t0, t1)
+            bank = psum.tile([P, t1 - t0], F32, name=f"score_bank{h}", tag=f"bank{h}" if h < 4 else "out_bank128")
             nc.tensor.matmul_mx(
                 out=bank[:],
                 lhsT=q_codes[:].bitcast(FP8X4),
                 lhsT_scale=q_scales[:],
-                rhs=k_words[:, 2 * h * HALF : 2 * (h + 1) * HALF].bitcast(FP4X4),
+                rhs=k_words[:, 2 * t0 : 2 * t1].bitcast(FP4X4),
                 rhs_scale=k_scales[:, cols],
                 start=True,
                 stop=True,
             )
             nc.scalar.activation(scores[:, cols], bank[:], ACT.Copy)
 
-        work = keep.tile([P, I + HALF], F32, align_bytes=64, tag="shared")
-        dist2 = (work[:, HALF:I], work[:, I:])
-        for h in (1, 0):
-            pos_listed = keep.tile([P, HALF], F32, align_bytes=64, name=f"pos_listed{h}", tag=("v_bf_a", "pos_b")[h])
-            nc.vector.tensor_copy(pos_listed[:], pos_all[:].indirect(offsets[:, h * HALF // 16 : (h + 1) * HALF // 16]))
-            nc.scalar.activation(dist2[h], pos_listed[:], ACT.Square, bias=qpos_col[:], scale=-1.0)
-        penalty = keep.tile([P, HALF], F32, align_bytes=64, tag="penalty")
-        nc.scalar.activation(penalty[:], dist2[1], ACT.Copy, scale=slope_col[:])
+        early = 384
+        pos_early = sb("pos_early", [P, early], F32, tag="scores_high")
+        nc.vector.tensor_copy(pos_early[:], pos_all[:].indirect(offsets[:, : early // 16]))
+        dist2 = sb("dist2", [P, I], F32)
+        dist2_low, dist2_high = dist2[:, :HALF], dist2[:, HALF:]
+        nc.scalar.activation(dist2[:, :early], pos_early[:], ACT.Square, bias=qpos_col[:], scale=-1.0)
+        scores_low = sb("scores_low", [P, HALF], F32)
+        nc.vector.tensor_copy(scores_low[:], listed(scores, 0))
+        neg_pos_late = sb("neg_pos_late", [P, I - early], F32, tag="v_bf_scalar")
+        nc.vector.tensor_tensor(
+            neg_pos_late[:], pos_all[:].indirect(offsets[:, early // 16 :]), minus_ones[:], ALU.mult
+        )
+        scores_high = sb("scores_high", [P, HALF], F32)
+        nc.scalar.activation(scores_high[:], listed(scores, 1), ACT.Copy)
+        nc.scalar.activation(dist2[:, early:], neg_pos_late[:], ACT.Square, bias=qpos_col[:], scale=1.0)
+        penalty_high = sb("penalty_high", [P, HALF], F32, tag="v_bf_pool")
+        nc.gpsimd.tensor_scalar(penalty_high[:], dist2_high, slope_col[:], 0.0, ALU.mult, ALU.add)
 
         fac_banks = []
         for g in range(passes):
@@ -146,71 +170,68 @@ def tile_attend_ownlists_positions_kernel(
                 nc.tensor.transpose(fac_bank[:, j, :], fac_cols[:, g, j : j + 1].to_broadcast([P, P]), ident[:])
             fac_banks.append(fac_bank)
 
-        v_bf = {}
-        v_codes = {}
-        v_scales = [keep.tile([P, E], U8, align_bytes=64, name=f"v_scales{g}") for g in range(passes)]
-
-        def cast_values(g, c0, dst, skip=0):
-            nc.scalar.copy(
-                out=dst.rearrange("p (c i) j -> p c j i", i=4),
-                in_=v_raw[g, c0][:, :, skip : skip + dst.shape[1]].rearrange("p j (c i) -> p c j i", i=4),
-            )
-
-        s = work[:, :I]
-        scores_listed = keep.tile([P, I], F32)
-        for h in range(2):
-            nc.vector.tensor_copy(
-                scores_listed[:, h * HALF : (h + 1) * HALF],
-                scores[:].indirect(offsets[:, h * HALF // 16 : (h + 1) * HALF // 16]),
-            )
+        costs = sb("costs", [P, I], F32)
         for c0, c1 in ((0, FIRST), (FIRST, HALF)):
             nc.vector.scalar_tensor_tensor(
-                out=s[:, c0:c1],
-                in0=dist2[0][:, c0:c1],
+                out=costs[:, c0:c1],
+                in0=dist2_low[:, c0:c1],
                 scalar=slope_col[:],
-                in1=scores_listed[:, c0:c1],
+                in1=scores_low[:, c0:c1],
                 op0=ALU.mult,
                 op1=ALU.subtract,
             )
-        nc.gpsimd.tensor_tensor(out=s[:, HALF:], in0=penalty[:], in1=scores_listed[:, HALF:], op=ALU.subtract)
-        nc.vector.tensor_copy(w_full[:].indirect(offsets[:, : FIRST // 16]), s[:, :FIRST])
-        neg_max = keep.tile([P, 1], F32)
-        nc.vector.tensor_reduce(neg_max[:], s, AXIS.X, ALU.min)
-        nc.vector.tensor_copy(w_full[:].indirect(offsets[:, FIRST // 16 :]), s[:, FIRST:])
-        v_bf_early = keep.tile([P, E + LATE, PACK], BF16, align_bytes=64, tag="v_bf_a")
-        v_bf[0, 0] = keep.tile([P, HEAD, PACK], BF16, align_bytes=64, name="v_bf_first", tag="penalty")
-        nc.gpsimd.tensor_copy(out=v_bf[0, 0][:], in_=v_raw[0, 0][:, :, :HEAD].rearrange("p j e -> p e j"))
-        v_bf[0, HEAD] = v_bf_early[:, HEAD:E, :]
-        cast_values(0, 0, v_bf_early[:, HEAD:HALF, :], HEAD)
-        cast_values(0, HALF, v_bf_early[:, HALF:E, :])
-        v_bf[1, 0] = v_bf_early[:, E : E + HALF, :]
-        cast_values(1, 0, v_bf[1, 0])
-        listed_exp = keep.tile([P, I], F32, align_bytes=64, tag="v_raw0_256")
-        row_sum = keep.tile([P, 1], F32)
-        nc.scalar.activation(listed_exp[:], s, ACT.Exp, bias=neg_max[:], scale=-1.0, accum_out=row_sum[:])
-        v_bf[1, HALF] = v_bf_early[:, E + HALF :, :]
-        cast_values(1, HALF, v_bf[1, HALF])
-        inv_sum = keep.tile([P, 1], F32)
+        nc.gpsimd.tensor_tensor(out=costs[:, HALF:], in0=penalty_high[:], in1=scores_high[:], op=ALU.subtract)
+        nc.vector.tensor_copy(w_full[:].indirect(offsets[:, : FIRST // 16]), costs[:, :FIRST])
+        least = sb("least", [P, 1], F32)
+        nc.vector.tensor_reduce(least[:], costs[:], AXIS.X, ALU.min)
+        nc.vector.tensor_copy(w_full[:].indirect(offsets[:, FIRST // 16 :]), costs[:, FIRST:])
+
+        v_bf = {}
+        v_codes = {}
+        v_scales = [sb(f"v_scales{g}", [P, E], U8) for g in range(passes)]
+
+        def cast_values(engine, g, c0, c1, dst):
+            base = c0 // HALF * HALF
+            src = v_raw[g, base][:, :, c0 - base : c1 - base]
+            v_bf[g, c0] = dst
+            if engine == "scalar":
+                nc.scalar.copy(
+                    out=dst.rearrange("p (c i) j -> p c j i", i=4), in_=src.rearrange("p j (c i) -> p c j i", i=4)
+                )
+            else:
+                nc.gpsimd.tensor_copy(out=dst, in_=src.rearrange("p j e -> p e j"))
+
+        by_scalar = sb("v_bf_scalar", [P, 384, PACK], BF16)
+        by_pool = sb("v_bf_pool", [P, 384, PACK], BF16)
+        cast_values("scalar", 0, 0, HALF, by_scalar[:, :HALF, :])
+        cast_values("scalar", 0, HALF, 384, by_scalar[:, HALF:, :])
+        cast_values("pool", 0, 384, E, by_pool[:, :128, :])
+        cast_values("pool", 1, 0, HALF, by_pool[:, 128:, :])
+        listed_exp = at(0, "listed_exp", [P, 4 * I], F32)
+        row_sum = sb("row_sum", [P, 1], F32)
+        nc.scalar.activation(listed_exp[:, :I], costs[:], ACT.Exp, bias=least[:], scale=-1.0, accum_out=row_sum[:])
+        after_sum = at(0, "v_bf_after_sum", [P, 192, PACK], BF16)
+        cast_values("scalar", 1, HALF, HALF + 192, after_sum[:])
+        inv_sum = sb("inv_sum", [P, 1], F32)
         nc.vector.reciprocal(inv_sum[:], row_sum[:])
 
         def quantise_values(g, c0, c1):
             bf_c0 = max(c for gg, c in v_bf if gg == g and c <= c0)
-            codes_c0 = max(c for gg, c in v_codes if gg == g and c <= c0)
             nc.vector.quantize_mx(
-                out=v_codes[g, codes_c0][:, c0 - codes_c0 : c1 - codes_c0].bitcast(FP8X4),
+                out=v_codes[g][:, c0:c1].bitcast(FP8X4),
                 scales=v_scales[g][:, c0:c1],
                 in_=v_bf[g, bf_c0][:, c0 - bf_c0 : c1 - bf_c0, :].rearrange("p e j -> p (e j)"),
             )
 
-        v_codes[0, 0] = keep.tile([P, E], U32, align_bytes=64, name="v_codes_0", tag="v_raw0_256")
-        for c0, c1 in ((HALF, E), (HEAD, HALF), (0, HEAD)):
+        v_codes[0] = at(2048, "v_codes0", [P, E], U32)
+        for c0, c1 in ((0, HALF), (HALF, 384), (384, E)):
             quantise_values(0, c0, c1)
 
-        p_early = keep.tile([P, 3, HALF], F32, align_bytes=64)
-        p_last = keep.tile([P, HALF], F32, align_bytes=64, tag="shared")
+        p_early = at(4096, "p_early", [P, 3, HALF], F32)
+        p_last = at(7168, "p_last", [P, HALF], F32)
         w_t = []
         for g in range(passes):
-            w_bf = keep.tile([P, K_PASS], BF16, align_bytes=64, name=f"w_bf{g}")
+            w_bf = sb(f"w_bf{g}", [P, K_PASS], BF16)
             turned = psum.tile([P, 2, Q], F32, name=f"turned{g}", tag=f"bank{g}")
             w_pass = w_full[:, g * K_PASS : (g + 1) * K_PASS].rearrange("q (p j) -> q p j", j=PACK)
             for u in range(2):
@@ -221,7 +242,7 @@ def tile_attend_ownlists_positions_kernel(
                 for p0, p1 in zip(cuts, cuts[1:]):
                     p_pair = p_piece[:, 2 * p0 : 2 * p1].rearrange("q (p e) -> q p e", e=2)
                     nc.scalar.activation(
-                        p_pair, w_pass[:, p0:p1, 2 * u : 2 * u + 2], ACT.Exp, bias=neg_max[:], scale=-1.0
+                        p_pair, w_pass[:, p0:p1, 2 * u : 2 * u + 2], ACT.Exp, bias=least[:], scale=-1.0
                     )
                     nc.vector.scalar_tensor_tensor(
                         out=pair[:, 2 * p0 : 2 * p1].rearrange("q (p e) -> q p e", e=2),
@@ -232,10 +253,10 @@ def tile_attend_ownlists_positions_kernel(
                         op1=ALU.mult,
                     )
                 nc.tensor.transpose(turned[:, u, :], pair.bitcast(F32), ident[:])
-            w_t.append((turned, keep.tile([P, Q * PACK], BF16, align_bytes=64, name=f"w_t{g}")))
+            w_t.append((turned, sb(f"w_t{g}", [P, Q * PACK], BF16)))
 
-        v_codes[1, 0] = keep.tile([P, E], U32, align_bytes=64, name="v_codes_1", tag="p_early")
-        for c0, c1 in ((0, HALF), (HALF, LAST), (LAST, LATE)):
+        v_codes[1] = at(4096, "v_codes1", [P, E], U32)
+        for c0, c1 in ((0, HALF), (HALF, HALF + 128), (HALF + 128, HALF + 192)):
             quantise_values(1, c0, c1)
 
         w_codes = []
@@ -247,8 +268,8 @@ def tile_attend_ownlists_positions_kernel(
                     out=w_tg[:].bitcast(F32).rearrange("p (q u) -> p q u", u=2)[:, rows, :],
                     in_=turned[:, :, rows].rearrange("p u q -> p q u"),
                 )
-            codes = keep.tile([P, Q], U32, align_bytes=64, name=f"w_codes{g}")
-            scales = keep.tile([P, Q], U8, align_bytes=64, name=f"w_scales{g}")
+            codes = sb(f"w_codes{g}", [P, Q], U32)
+            scales = sb(f"w_scales{g}", [P, Q], U8)
             for rows in q_halves:
                 nc.vector.quantize_mx(
                     out=codes[:, rows].bitcast(FP8X4),
@@ -258,25 +279,24 @@ def tile_attend_ownlists_positions_kernel(
             w_codes.append(codes)
             w_scales.append(scales)
             if g == 0:
-                v_bf[1, LATE] = keep.tile([P, E - LATE, PACK], BF16, align_bytes=64, name="v_bf_last", tag="w_bf0")
-                cast_values(1, HALF, v_bf[1, LATE][:], LATE - HALF)
-        quantise_values(1, LATE, E)
+                late = sb("v_bf_late", [P, 64, PACK], BF16, tag="w_bf0")
+                cast_values("scalar", 1, HALF + 192, E, late[:])
+        quantise_values(1, HALF + 192, E)
 
         pieces = [(c0, c0 + P) for c0 in range(0, E, P)]
         out_banks = [psum.tile([P, c1 - c0], F32, name=f"out_bank{c0}") for c0, c1 in pieces]
         for g in range(passes):
             for bank, (c0, c1) in zip(out_banks, pieces):
-                codes_c0 = max(c for gg, c in v_codes if gg == g and c <= c0)
                 nc.tensor.matmul_mx(
                     out=bank[:],
                     lhsT=w_codes[g][:].bitcast(FP8X4),
                     lhsT_scale=w_scales[g][:],
-                    rhs=v_codes[g, codes_c0][:, c0 - codes_c0 : c1 - codes_c0].bitcast(FP8X4),
+                    rhs=v_codes[g][:, c0:c1].bitcast(FP8X4),
                     rhs_scale=v_scales[g][:, c0:c1],
                     start=(g == 0),
                     stop=(g == passes - 1),
                 )
-        result = keep.tile([P, E], F32)
+        result = sb("result", [P, E], F32)
         for n, (bank, (c0, c1)) in enumerate(zip(out_banks, pieces)):
             if n % 2 == 0:
                 nc.scalar.copy(out=result[:, c0:c1], in_=bank[:])

@@ -21,7 +21,7 @@ P = 128
 PACK = 4
 K_PASS = P * PACK
 HALF = 256
-FIRST = 192
+QUARTER = 128
 UNLISTED = 2.0**100
 
 
@@ -36,57 +36,61 @@ def tile_attend_ownlists_positions_kernel(
         laid = ctx.enter_context(tc.tile_pool(name="laid", bufs=1))
         psum = ctx.enter_context(tc.psum_pool(name="psum", bufs=1))
 
-        def sb(name, shape, dtype, tag=None):
-            return keep.tile(shape, dtype, name=name, tag=tag or name, align_bytes=64)
+        def sb(name, shape, dtype):
+            return keep.tile(shape, dtype, name=name, tag=name, align_bytes=64)
 
         def at(offset, name, shape, dtype):
             return laid.tile(shape, dtype, name=name, tag=name, align_bytes=64, offset=offset)
 
+        def bank(n, name, shape):
+            return psum.tile(shape, F32, name=name, tag=f"bank{n}")
+
+        PEN, EXPS, RAW, IDENT, LISTED = 0, 4096, 8192, 12288, 12800
+
         pos_cols = sb("pos_cols", [P, PACK], F32)
         nc.sync.dma_start(out=pos_cols[:], in_=pos[0:1, K_PASS:].rearrange("o (p j) -> p (o j)", j=PACK))
+        k_scales = sb("k_scales", [P, 4 * T], U8)
+        k_scale_words = k_scales[:].bitcast(I32)
+        nc.sync.dma_start(
+            out=k_scale_words[0:4, :].rearrange("r (g c) -> r g c", g=4),
+            in_=keys_scales[0].bitcast(I32).rearrange("(g r) c -> r g c", r=4),
+        )
         q_raw = sb("q_raw", [P, PACK, Q], F32)
         nc.sync.dma_start(out=q_raw[:], in_=query.rearrange("(p j) q -> p j q", j=PACK))
-        k_scales = sb("k_scales", [P, T], U8)
-        for quad in range(4):
-            nc.sync.dma_start(
-                out=k_scales[32 * quad : 32 * quad + 4, :].bitcast(I32),
-                in_=keys_scales[0, 4 * quad : 4 * quad + 4, :].bitcast(I32),
-            )
-        k_words = sb("k_words", [P, 2 * T], U8, tag="costs")
-        nc.sync.dma_start(out=k_words[:].bitcast(I32), in_=keys_words[0].bitcast(I32))
-        pos_all = sb("pos_all", [P, T], F32)
-        nc.sync.dma_start(out=pos_all[:, :K_PASS], in_=pos[:, :K_PASS])
-        offsets = keep.tile([P, I // 16], U16)
-        nc.sync.dma_start(offsets[:], offs)
-        v_raw = {}
-
-        def load_values(g, c0):
-            if (g, c0) == (0, HALF):
-                v_raw[g, c0] = at(0, f"v_raw{g}_{c0}", [P, PACK, HALF], F32)
-            else:
-                v_raw[g, c0] = sb(f"v_raw{g}_{c0}", [P, PACK, HALF], F32)
-            nc.sync.dma_start(
-                out=v_raw[g, c0][:],
-                in_=vals[g * K_PASS : (g + 1) * K_PASS, c0 : c0 + HALF].rearrange("(p j) e -> p j e", j=PACK),
-            )
-
         qpos_col = sb("qpos_col", [P, 1], F32)
         nc.sync.dma_start(out=qpos_col[:], in_=qpos)
+        offsets = keep.tile([P, I // 16], U16)
+        nc.sync.dma_start(offsets[:], offs)
+        pos_all = sb("pos_all", [P, T], F32)
+        nc.sync.dma_start(out=pos_all[:, :K_PASS], in_=pos[:, :K_PASS])
+        k_words = [sb(f"k_words{g}", [P, 2 * K_PASS], U8) for g in range(passes)]
+        for g in range(passes):
+            nc.sync.dma_start(
+                out=k_words[g][:].bitcast(I32), in_=keys_words[0].bitcast(I32)[:, g * HALF : (g + 1) * HALF]
+            )
         slope_col = sb("slope_col", [P, 1], F32)
         nc.sync.dma_start(out=slope_col[:], in_=slope)
-        load_values(0, 0)
-        load_values(0, HALF)
+        v_raw = {}
+
+        def load_values(g, c0, c1, tile):
+            v_raw[g, c0] = tile
+            nc.sync.dma_start(
+                out=tile[:], in_=vals[g * K_PASS : (g + 1) * K_PASS, c0:c1].rearrange("(p j) e -> p j e", j=PACK)
+            )
+
+        load_values(0, 0, HALF, sb("v_raw0_low", [P, PACK, HALF], F32))
+        load_values(0, HALF, E, sb("v_raw0_high", [P, PACK, HALF], F32))
         fac_cols = sb("fac_cols", [P, passes, PACK], F32)
         nc.sync.dma_start(out=fac_cols[:], in_=fac.rearrange("o (g p j) -> p (o g) j", g=passes, j=PACK))
-        load_values(1, 0)
-        load_values(1, HALF)
+        load_values(1, 0, HALF, sb("v_raw1_low", [P, PACK, HALF], F32))
+        load_values(1, HALF, E, at(RAW, "v_raw1_high", [P, PACK, HALF], F32))
 
-        def listed(window, half):
-            return window[:].indirect(offsets[:, half * HALF // 16 : (half + 1) * HALF // 16])
+        def listed(window, slots):
+            return window[:].indirect(offsets[:, slots.start // 16 : slots.stop // 16])
 
-        zeros = sb("zeros", [P, P], F32, tag="w_full")
+        zeros = sb("zeros", [P, P], F32)
         nc.gpsimd.memset(zeros[:], 0.0)
-        ident_first = sb("ident_first", [P, P], F32, tag="q_codes")
+        ident_first = at(IDENT, "ident_first", [P, P], F32)
         ident = sb("ident", [P, P], F32)
         for tile in (ident_first, ident):
             nc.gpsimd.affine_select(
@@ -98,13 +102,23 @@ def tile_attend_ownlists_positions_kernel(
                 pattern=[[-1, P]],
                 channel_multiplier=1,
             )
-        w_full = sb("w_full", [P, T], F32)
-        nc.gpsimd.memset(w_full[:], UNLISTED)
+        minus_one = sb("minus_one", [P, 1], F32)
+        nc.gpsimd.memset(minus_one[:], -1.0)
+        cost_full = sb("cost_full", [P, T], F32)
+        nc.gpsimd.memset(cost_full[:], UNLISTED)
 
-        minus_ones = sb("minus_ones", [P, P], F32)
-        nc.gpsimd.memset(minus_ones[:], -1.0)
+        for g in range(1, 4):
+            nc.vector.tensor_copy(
+                out=k_scale_words[32 * g : 32 * g + 4, : T // 4], in_=k_scale_words[0:4, g * T // 4 : (g + 1) * T // 4]
+            )
 
-        pos_bank = psum.tile([P, PACK, P], F32, tag="out_bank0")
+        q_bf = sb("q_bf", [P, Q, PACK], BF16)
+        q_halves = [slice(0, Q // 2), slice(Q // 2, Q)]
+        nc.vector.tensor_copy(
+            out=q_bf[:].rearrange("p (c i) j -> p c j i", i=4), in_=q_raw[:].rearrange("p j (c i) -> p c j i", i=4)
+        )
+
+        pos_bank = bank(0, "pos_bank", [P, PACK, P])
         for j in range(PACK):
             nc.tensor.transpose(
                 pos_bank[:, j, :], pos_cols[:, j : j + 1].to_broadcast([P, P]), (ident if j else ident_first)[:]
@@ -113,127 +127,98 @@ def tile_attend_ownlists_positions_kernel(
             pos_all[:, K_PASS:].rearrange("q (p j) -> q p j", j=PACK), pos_bank[:].rearrange("q j p -> q p j"), ACT.Copy
         )
 
-        q_bf = sb("q_bf", [P, Q, PACK], BF16)
-        q_halves = [slice(0, Q // 2), slice(Q // 2, Q)]
-        nc.vector.tensor_copy(out=q_bf[:, :64, :], in_=q_raw[:, :, :64].rearrange("p j q -> p q j"))
-        nc.scalar.copy(
-            out=q_bf[:, 64:, :].rearrange("p (c i) j -> p c j i", i=4),
-            in_=q_raw[:, :, 64:].rearrange("p j (c i) -> p c j i", i=4),
-        )
-        q_codes = sb("q_codes", [P, Q], U32)
+        q_codes = at(IDENT, "q_codes", [P, Q], U32)
         q_scales = sb("q_scales", [P, Q], U8)
-        for rows in q_halves:
-            nc.vector.quantize_mx(
-                out=q_codes[:, rows].bitcast(FP8X4),
-                scales=q_scales[:, rows],
-                in_=q_bf[:, rows, :].rearrange("p q j -> p (q j)"),
-            )
+        qpos_row = sb("qpos_row", [P, HALF], F32)
+        nc.vector.tensor_copy(out=qpos_row[:], in_=qpos_col[:].to_broadcast([P, HALF]))
+        nc.vector.quantize_mx(
+            out=q_codes[:].bitcast(FP8X4), scales=q_scales[:], in_=q_bf[:].rearrange("p q j -> p (q j)")
+        )
 
         scores = sb("scores", [P, T], F32)
-        cuts = (0, 128, 384, 640, 896, T)
+        cuts = (0, 128, 384, 512, 768, 896, T)
         for h, (t0, t1) in enumerate(zip(cuts, cuts[1:])):
             cols = slice(t0, t1)
-            bank = psum.tile([P, t1 - t0], F32, name=f"score_bank{h}", tag=f"bank{h}" if h < 4 else "out_bank128")
+            score_bank = bank((1, 2, 3, 4, 5, 6)[h], f"score_bank{h}", [P, t1 - t0])
             nc.tensor.matmul_mx(
-                out=bank[:],
+                out=score_bank[:],
                 lhsT=q_codes[:].bitcast(FP8X4),
                 lhsT_scale=q_scales[:],
-                rhs=k_words[:, 2 * t0 : 2 * t1].bitcast(FP4X4),
+                rhs=k_words[t0 // K_PASS][:, 2 * (t0 % K_PASS) : 2 * (t0 % K_PASS + t1 - t0)].bitcast(FP4X4),
                 rhs_scale=k_scales[:, cols],
                 start=True,
                 stop=True,
             )
-            nc.scalar.activation(scores[:, cols], bank[:], ACT.Copy)
-
-        early = 384
-        pos_early = sb("pos_early", [P, early], F32, tag="scores_high")
-        nc.vector.tensor_copy(pos_early[:], pos_all[:].indirect(offsets[:, : early // 16]))
-        dist2 = sb("dist2", [P, I], F32)
-        dist2_low, dist2_high = dist2[:, :HALF], dist2[:, HALF:]
-        nc.scalar.activation(dist2[:, :early], pos_early[:], ACT.Square, bias=qpos_col[:], scale=-1.0)
-        scores_low = sb("scores_low", [P, HALF], F32)
-        nc.vector.tensor_copy(scores_low[:], listed(scores, 0))
-        neg_pos_late = sb("neg_pos_late", [P, I - early], F32, tag="v_bf_scalar")
-        nc.vector.tensor_tensor(
-            neg_pos_late[:], pos_all[:].indirect(offsets[:, early // 16 :]), minus_ones[:], ALU.mult
-        )
-        scores_high = sb("scores_high", [P, HALF], F32)
-        nc.scalar.activation(scores_high[:], listed(scores, 1), ACT.Copy)
-        nc.scalar.activation(dist2[:, early:], neg_pos_late[:], ACT.Square, bias=qpos_col[:], scale=1.0)
-        penalty_high = sb("penalty_high", [P, HALF], F32, tag="v_bf_pool")
-        nc.gpsimd.tensor_scalar(penalty_high[:], dist2_high, slope_col[:], 0.0, ALU.mult, ALU.add)
+            nc.scalar.activation(scores[:, cols], score_bank[:], ACT.Copy)
 
         fac_banks = []
         for g in range(passes):
-            fac_bank = psum.tile([P, PACK, P], F32, name=f"fac_bank{g}", tag=f"bank{2 + g}")
+            fac_bank = bank(4 + g, f"fac_bank{g}", [P, PACK, P])
             for j in range(PACK):
                 nc.tensor.transpose(fac_bank[:, j, :], fac_cols[:, g, j : j + 1].to_broadcast([P, P]), ident[:])
             fac_banks.append(fac_bank)
 
-        costs = sb("costs", [P, I], F32)
-        for c0, c1 in ((0, FIRST), (FIRST, HALF)):
+        halves = [slice(0, HALF), slice(HALF, I)]
+        dist = sb("dist", [P, I], F32)
+        for slots in halves:
+            nc.vector.tensor_tensor(dist[:, slots], listed(pos_all, slots), qpos_row[:], ALU.subtract)
+        penalty = at(PEN, "penalty", [P, I], F32)
+        for slots in halves:
             nc.vector.scalar_tensor_tensor(
-                out=costs[:, c0:c1],
-                in0=dist2_low[:, c0:c1],
+                out=penalty[:, slots],
+                in0=dist[:, slots],
                 scalar=slope_col[:],
-                in1=scores_low[:, c0:c1],
+                in1=dist[:, slots],
                 op0=ALU.mult,
-                op1=ALU.subtract,
+                op1=ALU.mult,
             )
-        nc.gpsimd.tensor_tensor(out=costs[:, HALF:], in0=penalty_high[:], in1=scores_high[:], op=ALU.subtract)
-        nc.vector.tensor_copy(w_full[:].indirect(offsets[:, : FIRST // 16]), costs[:, :FIRST])
-        least = sb("least", [P, 1], F32)
-        nc.vector.tensor_reduce(least[:], costs[:], AXIS.X, ALU.min)
-        nc.vector.tensor_copy(w_full[:].indirect(offsets[:, FIRST // 16 :]), costs[:, FIRST:])
+        s_listed = at(LISTED, "s_listed", [P, I], F32)
+        for slots in halves:
+            nc.vector.tensor_tensor(s_listed[:, slots], listed(scores, slots), penalty[:, slots], ALU.subtract)
+        nc.scalar.activation(listed(cost_full, halves[0]), s_listed[:, halves[0]], ACT.Copy, scale=minus_one[:])
 
-        v_bf = {}
-        v_codes = {}
-        v_scales = [sb(f"v_scales{g}", [P, E], U8) for g in range(passes)]
-
-        def cast_values(engine, g, c0, c1, dst):
-            base = c0 // HALF * HALF
+        def cast_values(g, c0, c1, dst):
+            base = max(c for gg, c in v_raw if gg == g and c <= c0)
             src = v_raw[g, base][:, :, c0 - base : c1 - base]
-            v_bf[g, c0] = dst
-            if engine == "scalar":
-                nc.scalar.copy(
-                    out=dst.rearrange("p (c i) j -> p c j i", i=4), in_=src.rearrange("p j (c i) -> p c j i", i=4)
-                )
-            else:
-                nc.gpsimd.tensor_copy(out=dst, in_=src.rearrange("p j e -> p e j"))
-
-        by_scalar = sb("v_bf_scalar", [P, 384, PACK], BF16)
-        by_pool = sb("v_bf_pool", [P, 384, PACK], BF16)
-        cast_values("scalar", 0, 0, HALF, by_scalar[:, :HALF, :])
-        cast_values("scalar", 0, HALF, 384, by_scalar[:, HALF:, :])
-        cast_values("pool", 0, 384, E, by_pool[:, :128, :])
-        cast_values("pool", 1, 0, HALF, by_pool[:, 128:, :])
-        listed_exp = at(0, "listed_exp", [P, 4 * I], F32)
-        row_sum = sb("row_sum", [P, 1], F32)
-        nc.scalar.activation(listed_exp[:, :I], costs[:], ACT.Exp, bias=least[:], scale=-1.0, accum_out=row_sum[:])
-        after_sum = at(0, "v_bf_after_sum", [P, 192, PACK], BF16)
-        cast_values("scalar", 1, HALF, HALF + 192, after_sum[:])
-        inv_sum = sb("inv_sum", [P, 1], F32)
-        nc.vector.reciprocal(inv_sum[:], row_sum[:])
+            nc.vector.tensor_copy(
+                out=dst[:, c0:c1, :].rearrange("p (c i) j -> p c j i", i=4),
+                in_=src.rearrange("p j (c i) -> p c j i", i=4),
+            )
 
         def quantise_values(g, c0, c1):
-            bf_c0 = max(c for gg, c in v_bf if gg == g and c <= c0)
             nc.vector.quantize_mx(
-                out=v_codes[g][:, c0:c1].bitcast(FP8X4),
+                out=v_codes[g, c0][:].bitcast(FP8X4),
                 scales=v_scales[g][:, c0:c1],
-                in_=v_bf[g, bf_c0][:, c0 - bf_c0 : c1 - bf_c0, :].rearrange("p e j -> p (e j)"),
+                in_=v_bf[g][:, c0:c1, :].rearrange("p e j -> p (e j)"),
             )
 
-        v_codes[0] = at(2048, "v_codes0", [P, E], U32)
-        for c0, c1 in ((0, HALF), (HALF, 384), (384, E)):
-            quantise_values(0, c0, c1)
+        v_bf = [at(PEN, "v_bf0", [P, E, PACK], BF16), at(LISTED, "v_bf1", [P, E, PACK], BF16)]
+        v_codes = {key: sb(f"v_codes{key[0]}", [P, E >> key[0]], U32) for key in ((0, 0), (1, 0))}
+        v_scales = [sb(f"v_scales{g}", [P, E], U8) for g in range(passes)]
+        cast_values(0, 0, QUARTER, v_bf[0])
+        costs = sb("costs", [P, I], F32)
+        least = sb("least", [P, 1], F32)
+        nc.vector.tensor_scalar(costs[:], s_listed[:], -1.0, None, ALU.mult, ALU.min, accum_out=least[:])
+        listed_exp = sb("listed_exp", [P, I], F32)
+        row_sum = sb("row_sum", [P, 1], F32)
+        nc.scalar.activation(listed_exp[:], costs[:], ACT.Exp, bias=least[:], scale=-1.0, accum_out=row_sum[:])
+        nc.scalar.activation(listed(cost_full, halves[1]), costs[:, halves[1]], ACT.Copy)
+        cast_values(0, QUARTER, HALF, v_bf[0])
+        cast_values(0, HALF, E, v_bf[0])
+        inv_sum = sb("inv_sum", [P, 1], F32)
+        nc.vector.reciprocal(inv_sum[:], row_sum[:])
+        cast_values(1, 0, HALF, v_bf[1])
+        quantise_values(0, 0, E)
+        quantise_values(1, 0, HALF)
+        cast_values(1, HALF, E, v_bf[1])
 
-        p_early = at(4096, "p_early", [P, 3, HALF], F32)
-        p_last = at(7168, "p_last", [P, HALF], F32)
+        p_early = at(EXPS, "p_early", [P, 3, HALF], F32)
+        p_last = sb("p_last", [P, HALF], F32)
         w_t = []
         for g in range(passes):
-            w_bf = sb(f"w_bf{g}", [P, K_PASS], BF16)
-            turned = psum.tile([P, 2, Q], F32, name=f"turned{g}", tag=f"bank{g}")
-            w_pass = w_full[:, g * K_PASS : (g + 1) * K_PASS].rearrange("q (p j) -> q p j", j=PACK)
+            w_bf = at(RAW + 1024 * g, f"w_bf{g}", [P, K_PASS], BF16)
+            turned = bank(1 + g, f"turned{g}", [P, 2, Q])
+            cost_pass = cost_full[:, g * K_PASS : (g + 1) * K_PASS].rearrange("q (p j) -> q p j", j=PACK)
             for u in range(2):
                 pair = w_bf[:, u * HALF : (u + 1) * HALF]
                 last = (g, u) == (passes - 1, 1)
@@ -242,7 +227,7 @@ def tile_attend_ownlists_positions_kernel(
                 for p0, p1 in zip(cuts, cuts[1:]):
                     p_pair = p_piece[:, 2 * p0 : 2 * p1].rearrange("q (p e) -> q p e", e=2)
                     nc.scalar.activation(
-                        p_pair, w_pass[:, p0:p1, 2 * u : 2 * u + 2], ACT.Exp, bias=least[:], scale=-1.0
+                        p_pair, cost_pass[:, p0:p1, 2 * u : 2 * u + 2], ACT.Exp, bias=least[:], scale=-1.0
                     )
                     nc.vector.scalar_tensor_tensor(
                         out=pair[:, 2 * p0 : 2 * p1].rearrange("q (p e) -> q p e", e=2),
@@ -255,9 +240,8 @@ def tile_attend_ownlists_positions_kernel(
                 nc.tensor.transpose(turned[:, u, :], pair.bitcast(F32), ident[:])
             w_t.append((turned, sb(f"w_t{g}", [P, Q * PACK], BF16)))
 
-        v_codes[1] = at(4096, "v_codes1", [P, E], U32)
-        for c0, c1 in ((0, HALF), (HALF, HALF + 128), (HALF + 128, HALF + 192)):
-            quantise_values(1, c0, c1)
+        v_codes[1, HALF] = at(EXPS, "v_codes_last", [P, HALF], U32)
+        quantise_values(1, HALF, E)
 
         w_codes = []
         w_scales = []
@@ -278,28 +262,25 @@ def tile_attend_ownlists_positions_kernel(
                 )
             w_codes.append(codes)
             w_scales.append(scales)
-            if g == 0:
-                late = sb("v_bf_late", [P, 64, PACK], BF16, tag="w_bf0")
-                cast_values("scalar", 1, HALF + 192, E, late[:])
-        quantise_values(1, HALF + 192, E)
 
-        pieces = [(c0, c0 + P) for c0 in range(0, E, P)]
-        out_banks = [psum.tile([P, c1 - c0], F32, name=f"out_bank{c0}") for c0, c1 in pieces]
+        pieces = list(range(0, E, P))
+        out_banks = [bank(b, f"out_bank{c0}", [P, P]) for b, c0 in zip((6, 7, 0, 3), pieces)]
         for g in range(passes):
-            for bank, (c0, c1) in zip(out_banks, pieces):
+            for out_bank, c0 in zip(out_banks, pieces):
+                base = max(c for gg, c in v_codes if gg == g and c <= c0)
                 nc.tensor.matmul_mx(
-                    out=bank[:],
+                    out=out_bank[:],
                     lhsT=w_codes[g][:].bitcast(FP8X4),
                     lhsT_scale=w_scales[g][:],
-                    rhs=v_codes[g][:, c0:c1].bitcast(FP8X4),
-                    rhs_scale=v_scales[g][:, c0:c1],
+                    rhs=v_codes[g, base][:, c0 - base : c0 - base + P].bitcast(FP8X4),
+                    rhs_scale=v_scales[g][:, c0 : c0 + P],
                     start=(g == 0),
                     stop=(g == passes - 1),
                 )
         result = sb("result", [P, E], F32)
-        for n, (bank, (c0, c1)) in enumerate(zip(out_banks, pieces)):
+        for n, (out_bank, c0) in enumerate(zip(out_banks, pieces)):
             if n % 2 == 0:
-                nc.scalar.copy(out=result[:, c0:c1], in_=bank[:])
+                nc.scalar.copy(out=result[:, c0 : c0 + P], in_=out_bank[:])
             else:
-                nc.vector.tensor_copy(out=result[:, c0:c1], in_=bank[:])
-            (nc.scalar, nc.sync, nc.scalar, nc.sync)[n].dma_start(out=out[:, c0:c1], in_=result[:, c0:c1])
+                nc.vector.tensor_copy(out=result[:, c0 : c0 + P], in_=out_bank[:])
+            (nc.scalar, nc.sync)[n % 2].dma_start(out=out[:, c0 : c0 + P], in_=result[:, c0 : c0 + P])

@@ -49,25 +49,22 @@ def tile_attend_ownlists_positions_kernel(
 
         pos_cols = sb("pos_cols", [P, PACK], F32)
         nc.sync.dma_start(out=pos_cols[:], in_=pos[0:1, K_PASS:].rearrange("o (p j) -> p (o j)", j=PACK))
-        k_scales = sb("k_scales", [P, 4 * T], U8)
-        k_scale_words = k_scales[:].bitcast(I32)
-        nc.sync.dma_start(
-            out=k_scale_words[0:4, :].rearrange("r (g c) -> r g c", g=4),
-            in_=keys_scales[0].bitcast(I32).rearrange("(g r) c -> r g c", r=4),
-        )
         q_raw = sb("q_raw", [P, PACK, Q], F32)
         nc.sync.dma_start(out=q_raw[:], in_=query.rearrange("(p j) q -> p j q", j=PACK))
-        qpos_col = sb("qpos_col", [P, 1], F32)
-        nc.sync.dma_start(out=qpos_col[:], in_=qpos)
-        offsets = keep.tile([P, I // 16], U16)
-        nc.sync.dma_start(offsets[:], offs)
+        k_scales = sb("k_scales", [P, T], U8)
+        for quad in range(4):
+            nc.sync.dma_start(
+                out=k_scales[32 * quad : 32 * quad + 4, :].bitcast(I32),
+                in_=keys_scales[0, 4 * quad : 4 * quad + 4, :].bitcast(I32),
+            )
+        k_words = at(LISTED, "k_words", [P, 2 * T], U8)
+        nc.sync.dma_start(out=k_words[:].bitcast(I32), in_=keys_words[0].bitcast(I32))
         pos_all = sb("pos_all", [P, T], F32)
         nc.sync.dma_start(out=pos_all[:, :K_PASS], in_=pos[:, :K_PASS])
-        k_words = [sb(f"k_words{g}", [P, 2 * K_PASS], U8) for g in range(passes)]
-        for g in range(passes):
-            nc.sync.dma_start(
-                out=k_words[g][:].bitcast(I32), in_=keys_words[0].bitcast(I32)[:, g * HALF : (g + 1) * HALF]
-            )
+        offsets = keep.tile([P, I // 16], U16)
+        nc.sync.dma_start(offsets[:], offs)
+        qpos_col = sb("qpos_col", [P, 1], F32)
+        nc.sync.dma_start(out=qpos_col[:], in_=qpos)
         slope_col = sb("slope_col", [P, 1], F32)
         nc.sync.dma_start(out=slope_col[:], in_=slope)
         v_raw = {}
@@ -102,21 +99,10 @@ def tile_attend_ownlists_positions_kernel(
                 pattern=[[-1, P]],
                 channel_multiplier=1,
             )
-        minus_one = sb("minus_one", [P, 1], F32)
-        nc.gpsimd.memset(minus_one[:], -1.0)
         cost_full = sb("cost_full", [P, T], F32)
         nc.gpsimd.memset(cost_full[:], UNLISTED)
-
-        for g in range(1, 4):
-            nc.vector.tensor_copy(
-                out=k_scale_words[32 * g : 32 * g + 4, : T // 4], in_=k_scale_words[0:4, g * T // 4 : (g + 1) * T // 4]
-            )
-
-        q_bf = sb("q_bf", [P, Q, PACK], BF16)
-        q_halves = [slice(0, Q // 2), slice(Q // 2, Q)]
-        nc.vector.tensor_copy(
-            out=q_bf[:].rearrange("p (c i) j -> p c j i", i=4), in_=q_raw[:].rearrange("p j (c i) -> p c j i", i=4)
-        )
+        minus_ones = sb("minus_ones", [P, P], F32)
+        nc.gpsimd.memset(minus_ones[:], -1.0)
 
         pos_bank = bank(0, "pos_bank", [P, PACK, P])
         for j in range(PACK):
@@ -127,24 +113,32 @@ def tile_attend_ownlists_positions_kernel(
             pos_all[:, K_PASS:].rearrange("q (p j) -> q p j", j=PACK), pos_bank[:].rearrange("q j p -> q p j"), ACT.Copy
         )
 
+        q_bf = sb("q_bf", [P, Q, PACK], BF16)
+        q_halves = [slice(0, Q // 2), slice(Q // 2, Q)]
+        nc.vector.tensor_copy(out=q_bf[:, :64, :], in_=q_raw[:, :, :64].rearrange("p j q -> p q j"))
+        nc.scalar.copy(
+            out=q_bf[:, 64:, :].rearrange("p (c i) j -> p c j i", i=4),
+            in_=q_raw[:, :, 64:].rearrange("p j (c i) -> p c j i", i=4),
+        )
         q_codes = at(IDENT, "q_codes", [P, Q], U32)
         q_scales = sb("q_scales", [P, Q], U8)
-        qpos_row = sb("qpos_row", [P, HALF], F32)
-        nc.vector.tensor_copy(out=qpos_row[:], in_=qpos_col[:].to_broadcast([P, HALF]))
-        nc.vector.quantize_mx(
-            out=q_codes[:].bitcast(FP8X4), scales=q_scales[:], in_=q_bf[:].rearrange("p q j -> p (q j)")
-        )
+        for rows in q_halves:
+            nc.vector.quantize_mx(
+                out=q_codes[:, rows].bitcast(FP8X4),
+                scales=q_scales[:, rows],
+                in_=q_bf[:, rows, :].rearrange("p q j -> p (q j)"),
+            )
 
         scores = sb("scores", [P, T], F32)
-        cuts = (0, 128, 384, 512, 768, 896, T)
+        cuts = (0, 128, 384, 640, 896, T)
         for h, (t0, t1) in enumerate(zip(cuts, cuts[1:])):
             cols = slice(t0, t1)
-            score_bank = bank((1, 2, 3, 4, 5, 6)[h], f"score_bank{h}", [P, t1 - t0])
+            score_bank = bank(1 + h, f"score_bank{h}", [P, t1 - t0])
             nc.tensor.matmul_mx(
                 out=score_bank[:],
                 lhsT=q_codes[:].bitcast(FP8X4),
                 lhsT_scale=q_scales[:],
-                rhs=k_words[t0 // K_PASS][:, 2 * (t0 % K_PASS) : 2 * (t0 % K_PASS + t1 - t0)].bitcast(FP4X4),
+                rhs=k_words[:, 2 * t0 : 2 * t1].bitcast(FP4X4),
                 rhs_scale=k_scales[:, cols],
                 start=True,
                 stop=True,
@@ -153,29 +147,35 @@ def tile_attend_ownlists_positions_kernel(
 
         fac_banks = []
         for g in range(passes):
-            fac_bank = bank(4 + g, f"fac_bank{g}", [P, PACK, P])
+            fac_bank = bank(3 + g, f"fac_bank{g}", [P, PACK, P])
             for j in range(PACK):
                 nc.tensor.transpose(fac_bank[:, j, :], fac_cols[:, g, j : j + 1].to_broadcast([P, P]), ident[:])
             fac_banks.append(fac_bank)
 
         halves = [slice(0, HALF), slice(HALF, I)]
-        dist = sb("dist", [P, I], F32)
-        for slots in halves:
-            nc.vector.tensor_tensor(dist[:, slots], listed(pos_all, slots), qpos_row[:], ALU.subtract)
-        penalty = at(PEN, "penalty", [P, I], F32)
-        for slots in halves:
+        early = 384
+        pos_early = at(EXPS, "pos_early", [P, early], F32)
+        nc.vector.tensor_copy(pos_early[:], listed(pos_all, slice(0, early)))
+        dist2 = at(PEN, "dist2", [P, I], F32)
+        nc.scalar.activation(dist2[:, :early], pos_early[:], ACT.Square, bias=qpos_col[:], scale=-1.0)
+        scores_low = sb("scores_low", [P, HALF], F32)
+        nc.vector.tensor_copy(scores_low[:], listed(scores, halves[0]))
+        neg_pos_late = sb("neg_pos_late", [P, I - early], F32)
+        nc.vector.tensor_tensor(neg_pos_late[:], listed(pos_all, slice(early, I)), minus_ones[:], ALU.mult)
+        scores_high = at(EXPS, "scores_high", [P, HALF], F32)
+        nc.scalar.activation(scores_high[:], listed(scores, halves[1]), ACT.Copy)
+        nc.scalar.activation(dist2[:, early:], neg_pos_late[:], ACT.Square, bias=qpos_col[:], scale=1.0)
+        costs_first = at(LISTED, "costs_first", [P, I], F32)
+        for slots, part in zip(halves, (scores_low, scores_high)):
             nc.vector.scalar_tensor_tensor(
-                out=penalty[:, slots],
-                in0=dist[:, slots],
+                out=costs_first[:, slots],
+                in0=dist2[:, slots],
                 scalar=slope_col[:],
-                in1=dist[:, slots],
+                in1=part[:],
                 op0=ALU.mult,
-                op1=ALU.mult,
+                op1=ALU.subtract,
             )
-        s_listed = at(LISTED, "s_listed", [P, I], F32)
-        for slots in halves:
-            nc.vector.tensor_tensor(s_listed[:, slots], listed(scores, slots), penalty[:, slots], ALU.subtract)
-        nc.scalar.activation(listed(cost_full, halves[0]), s_listed[:, halves[0]], ACT.Copy, scale=minus_one[:])
+        nc.scalar.activation(listed(cost_full, halves[0]), costs_first[:, halves[0]], ACT.Copy)
 
         def cast_values(g, c0, c1, dst):
             base = max(c for gg, c in v_raw if gg == g and c <= c0)
@@ -193,12 +193,12 @@ def tile_attend_ownlists_positions_kernel(
             )
 
         v_bf = [at(PEN, "v_bf0", [P, E, PACK], BF16), at(LISTED, "v_bf1", [P, E, PACK], BF16)]
-        v_codes = {key: sb(f"v_codes{key[0]}", [P, E >> key[0]], U32) for key in ((0, 0), (1, 0))}
+        v_codes = {key: sb(f"v_codes{key[0]}", [P, E >> key[0]], U32) for key in ((0, 0),)}
         v_scales = [sb(f"v_scales{g}", [P, E], U8) for g in range(passes)]
         cast_values(0, 0, QUARTER, v_bf[0])
         costs = sb("costs", [P, I], F32)
         least = sb("least", [P, 1], F32)
-        nc.vector.tensor_scalar(costs[:], s_listed[:], -1.0, None, ALU.mult, ALU.min, accum_out=least[:])
+        nc.vector.tensor_scalar(costs[:], costs_first[:], 1.0, None, ALU.mult, ALU.min, accum_out=least[:])
         listed_exp = sb("listed_exp", [P, I], F32)
         row_sum = sb("row_sum", [P, 1], F32)
         nc.scalar.activation(listed_exp[:], costs[:], ACT.Exp, bias=least[:], scale=-1.0, accum_out=row_sum[:])
@@ -209,7 +209,6 @@ def tile_attend_ownlists_positions_kernel(
         nc.vector.reciprocal(inv_sum[:], row_sum[:])
         cast_values(1, 0, HALF, v_bf[1])
         quantise_values(0, 0, E)
-        quantise_values(1, 0, HALF)
         cast_values(1, HALF, E, v_bf[1])
 
         p_early = at(EXPS, "p_early", [P, 3, HALF], F32)
@@ -240,8 +239,9 @@ def tile_attend_ownlists_positions_kernel(
                 nc.tensor.transpose(turned[:, u, :], pair.bitcast(F32), ident[:])
             w_t.append((turned, sb(f"w_t{g}", [P, Q * PACK], BF16)))
 
-        v_codes[1, HALF] = at(EXPS, "v_codes_last", [P, HALF], U32)
-        quantise_values(1, HALF, E)
+        for c0 in (0, HALF):
+            v_codes[1, c0] = at(EXPS + 4 * c0, f"v_codes1_{c0}", [P, HALF], U32)
+            quantise_values(1, c0, c0 + HALF)
 
         w_codes = []
         w_scales = []
@@ -264,7 +264,7 @@ def tile_attend_ownlists_positions_kernel(
             w_scales.append(scales)
 
         pieces = list(range(0, E, P))
-        out_banks = [bank(b, f"out_bank{c0}", [P, P]) for b, c0 in zip((6, 7, 0, 3), pieces)]
+        out_banks = [bank(b, f"out_bank{c0}", [P, P]) for b, c0 in zip((6, 7, 0, 5), pieces)]
         for g in range(passes):
             for out_bank, c0 in zip(out_banks, pieces):
                 base = max(c for gg, c in v_codes if gg == g and c <= c0)

@@ -21,7 +21,7 @@ P = 128
 PACK = 4
 K_PASS = P * PACK
 HALF = 256
-QUARTER = 128
+BY_POOL = 192
 UNLISTED = 2.0**100
 
 
@@ -45,7 +45,7 @@ def tile_attend_ownlists_positions_kernel(
         def bank(n, name, shape):
             return psum.tile(shape, F32, name=name, tag=f"bank{n}")
 
-        PEN, EXPS, RAW, IDENT, LISTED = 0, 4096, 8192, 12288, 12800
+        PEN, EXPS, RAW, IDENT, LISTED, SUMMED, LAST = 0, 4096, 8192, 12288, 12800, 16896, 20480
 
         pos_cols = sb("pos_cols", [P, PACK], F32)
         nc.sync.dma_start(out=pos_cols[:], in_=pos[0:1, K_PASS:].rearrange("o (p j) -> p (o j)", j=PACK))
@@ -76,11 +76,11 @@ def tile_attend_ownlists_positions_kernel(
             )
 
         load_values(0, 0, HALF, sb("v_raw0_low", [P, PACK, HALF], F32))
-        load_values(0, HALF, E, sb("v_raw0_high", [P, PACK, HALF], F32))
+        load_values(0, HALF, E, at(RAW, "v_raw0_high", [P, PACK, HALF], F32))
         fac_cols = sb("fac_cols", [P, passes, PACK], F32)
         nc.sync.dma_start(out=fac_cols[:], in_=fac.rearrange("o (g p j) -> p (o g) j", g=passes, j=PACK))
         load_values(1, 0, HALF, sb("v_raw1_low", [P, PACK, HALF], F32))
-        load_values(1, HALF, E, at(RAW, "v_raw1_high", [P, PACK, HALF], F32))
+        load_values(1, HALF, E, at(LAST, "v_raw1_high", [P, PACK, HALF], F32))
 
         def listed(window, slots):
             return window[:].indirect(offsets[:, slots.start // 16 : slots.stop // 16])
@@ -129,7 +129,7 @@ def tile_attend_ownlists_positions_kernel(
                 in_=q_bf[:, rows, :].rearrange("p q j -> p (q j)"),
             )
 
-        scores = sb("scores", [P, T], F32)
+        scores = at(PEN, "scores", [P, T], F32)
         cuts = (0, 128, 384, 640, 896, T)
         for h, (t0, t1) in enumerate(zip(cuts, cuts[1:])):
             cols = slice(t0, t1)
@@ -156,7 +156,7 @@ def tile_attend_ownlists_positions_kernel(
         early = 384
         pos_early = at(EXPS, "pos_early", [P, early], F32)
         nc.vector.tensor_copy(pos_early[:], listed(pos_all, slice(0, early)))
-        dist2 = at(PEN, "dist2", [P, I], F32)
+        dist2 = sb("dist2", [P, I], F32)
         nc.scalar.activation(dist2[:, :early], pos_early[:], ACT.Square, bias=qpos_col[:], scale=-1.0)
         scores_low = sb("scores_low", [P, HALF], F32)
         nc.vector.tensor_copy(scores_low[:], listed(scores, halves[0]))
@@ -165,57 +165,59 @@ def tile_attend_ownlists_positions_kernel(
         scores_high = at(EXPS, "scores_high", [P, HALF], F32)
         nc.scalar.activation(scores_high[:], listed(scores, halves[1]), ACT.Copy)
         nc.scalar.activation(dist2[:, early:], neg_pos_late[:], ACT.Square, bias=qpos_col[:], scale=1.0)
-        costs_first = at(LISTED, "costs_first", [P, I], F32)
+        costs = at(LISTED, "costs", [P, I], F32)
         for slots, part in zip(halves, (scores_low, scores_high)):
             nc.vector.scalar_tensor_tensor(
-                out=costs_first[:, slots],
+                out=costs[:, slots],
                 in0=dist2[:, slots],
                 scalar=slope_col[:],
                 in1=part[:],
                 op0=ALU.mult,
                 op1=ALU.subtract,
             )
-        nc.scalar.activation(listed(cost_full, halves[0]), costs_first[:, halves[0]], ACT.Copy)
+        nc.scalar.activation(listed(cost_full, halves[0]), costs[:, halves[0]], ACT.Copy)
 
-        def cast_values(g, c0, c1, dst):
-            base = max(c for gg, c in v_raw if gg == g and c <= c0)
+        def cast_values(engine, g, c0, c1, dst):
+            base = c0 // HALF * HALF
             src = v_raw[g, base][:, :, c0 - base : c1 - base]
-            nc.vector.tensor_copy(
-                out=dst[:, c0:c1, :].rearrange("p (c i) j -> p c j i", i=4),
-                in_=src.rearrange("p j (c i) -> p c j i", i=4),
-            )
+            if engine == "pool":
+                nc.gpsimd.tensor_copy(out=dst, in_=src.rearrange("p j e -> p e j"))
+            else:
+                copy = nc.scalar.copy if engine == "scalar" else nc.vector.tensor_copy
+                copy(out=dst.rearrange("p (c i) j -> p c j i", i=4), in_=src.rearrange("p j (c i) -> p c j i", i=4))
 
-        def quantise_values(g, c0, c1):
+        def quantise_values(g, c0, c1, src):
             nc.vector.quantize_mx(
-                out=v_codes[g, c0][:].bitcast(FP8X4),
+                out=v_codes[g][:, c0:c1].bitcast(FP8X4),
                 scales=v_scales[g][:, c0:c1],
-                in_=v_bf[g][:, c0:c1, :].rearrange("p e j -> p (e j)"),
+                in_=src.rearrange("p e j -> p (e j)"),
             )
 
-        v_bf = [at(PEN, "v_bf0", [P, E, PACK], BF16), at(LISTED, "v_bf1", [P, E, PACK], BF16)]
-        v_codes = {key: sb(f"v_codes{key[0]}", [P, E >> key[0]], U32) for key in ((0, 0),)}
+        v_bf0 = at(PEN, "v_bf0", [P, E, PACK], BF16)
+        v_codes = [sb("v_codes0", [P, E], U32)]
         v_scales = [sb(f"v_scales{g}", [P, E], U8) for g in range(passes)]
-        cast_values(0, 0, QUARTER, v_bf[0])
-        costs = sb("costs", [P, I], F32)
+        cast_values("vector", 0, 0, HALF, v_bf0[:, :HALF, :])
         least = sb("least", [P, 1], F32)
-        nc.vector.tensor_scalar(costs[:], costs_first[:], 1.0, None, ALU.mult, ALU.min, accum_out=least[:])
-        listed_exp = sb("listed_exp", [P, I], F32)
+        nc.vector.tensor_reduce(least[:], costs[:], AXIS.X, ALU.min)
+        listed_exp = at(SUMMED, "listed_exp", [P, I], F32)
         row_sum = sb("row_sum", [P, 1], F32)
         nc.scalar.activation(listed_exp[:], costs[:], ACT.Exp, bias=least[:], scale=-1.0, accum_out=row_sum[:])
-        nc.scalar.activation(listed(cost_full, halves[1]), costs[:, halves[1]], ACT.Copy)
-        cast_values(0, QUARTER, HALF, v_bf[0])
-        cast_values(0, HALF, E, v_bf[0])
+        cast_values("vector", 0, HALF, E, v_bf0[:, HALF:, :])
+        nc.vector.tensor_copy(listed(cost_full, halves[1]), costs[:, halves[1]])
+        v_bf_low = at(RAW, "v_bf_low", [P, HALF, PACK], BF16)
+        cast_values("pool", 1, 0, BY_POOL, v_bf_low[:, :BY_POOL, :])
+        cast_values("scalar", 1, BY_POOL, HALF, v_bf_low[:, BY_POOL:, :])
+        v_bf_high = at(SUMMED, "v_bf_high", [P, HALF, PACK], BF16)
+        cast_values("scalar", 1, HALF, E, v_bf_high[:])
+        quantise_values(0, 0, E, v_bf0[:])
         inv_sum = sb("inv_sum", [P, 1], F32)
         nc.vector.reciprocal(inv_sum[:], row_sum[:])
-        cast_values(1, 0, HALF, v_bf[1])
-        quantise_values(0, 0, E)
-        cast_values(1, HALF, E, v_bf[1])
 
-        p_early = at(EXPS, "p_early", [P, 3, HALF], F32)
-        p_last = sb("p_last", [P, HALF], F32)
+        p_early = at(LAST + 1024, "p_early", [P, 3, HALF], F32)
+        p_last = at(LAST, "p_last", [P, HALF], F32)
         w_t = []
         for g in range(passes):
-            w_bf = at(RAW + 1024 * g, f"w_bf{g}", [P, K_PASS], BF16)
+            w_bf = at(PEN + 1024 * g, f"w_bf{g}", [P, K_PASS], BF16)
             turned = bank(1 + g, f"turned{g}", [P, 2, Q])
             cost_pass = cost_full[:, g * K_PASS : (g + 1) * K_PASS].rearrange("q (p j) -> q p j", j=PACK)
             for u in range(2):
@@ -239,9 +241,9 @@ def tile_attend_ownlists_positions_kernel(
                 nc.tensor.transpose(turned[:, u, :], pair.bitcast(F32), ident[:])
             w_t.append((turned, sb(f"w_t{g}", [P, Q * PACK], BF16)))
 
-        for c0 in (0, HALF):
-            v_codes[1, c0] = at(EXPS + 4 * c0, f"v_codes1_{c0}", [P, HALF], U32)
-            quantise_values(1, c0, c0 + HALF)
+        v_codes.append(at(LAST + 1024, "v_codes1", [P, E], U32))
+        quantise_values(1, 0, HALF, v_bf_low[:])
+        quantise_values(1, HALF, E, v_bf_high[:])
 
         w_codes = []
         w_scales = []
@@ -267,12 +269,11 @@ def tile_attend_ownlists_positions_kernel(
         out_banks = [bank(b, f"out_bank{c0}", [P, P]) for b, c0 in zip((6, 7, 0, 5), pieces)]
         for g in range(passes):
             for out_bank, c0 in zip(out_banks, pieces):
-                base = max(c for gg, c in v_codes if gg == g and c <= c0)
                 nc.tensor.matmul_mx(
                     out=out_bank[:],
                     lhsT=w_codes[g][:].bitcast(FP8X4),
                     lhsT_scale=w_scales[g][:],
-                    rhs=v_codes[g, base][:, c0 - base : c0 - base + P].bitcast(FP8X4),
+                    rhs=v_codes[g][:, c0 : c0 + P].bitcast(FP8X4),
                     rhs_scale=v_scales[g][:, c0 : c0 + P],
                     start=(g == 0),
                     stop=(g == passes - 1),

@@ -21,7 +21,8 @@ P = 128
 PACK = 4
 K_PASS = P * PACK
 HALF = 256
-BY_POOL = 192
+QUARTER = 128
+FIRST = 160
 UNLISTED = 2.0**100
 
 
@@ -45,7 +46,7 @@ def tile_attend_ownlists_positions_kernel(
         def bank(n, name, shape):
             return psum.tile(shape, F32, name=name, tag=f"bank{n}")
 
-        PEN, EXPS, RAW, IDENT, LISTED, SUMMED, LAST = 0, 4096, 8192, 12288, 12800, 16896, 20480
+        PEN, EXPS, PICKED, IDENT, LISTED, SUMMED, LAST = 0, 4096, 8192, 12288, 12800, 16896, 22528
 
         pos_cols = sb("pos_cols", [P, PACK], F32)
         nc.sync.dma_start(out=pos_cols[:], in_=pos[0:1, K_PASS:].rearrange("o (p j) -> p (o j)", j=PACK))
@@ -76,11 +77,11 @@ def tile_attend_ownlists_positions_kernel(
             )
 
         load_values(0, 0, HALF, sb("v_raw0_low", [P, PACK, HALF], F32))
-        load_values(0, HALF, E, at(RAW, "v_raw0_high", [P, PACK, HALF], F32))
+        load_values(0, HALF, E, sb("v_raw0_high", [P, PACK, HALF], F32))
         fac_cols = sb("fac_cols", [P, passes, PACK], F32)
         nc.sync.dma_start(out=fac_cols[:], in_=fac.rearrange("o (g p j) -> p (o g) j", g=passes, j=PACK))
-        load_values(1, 0, HALF, sb("v_raw1_low", [P, PACK, HALF], F32))
-        load_values(1, HALF, E, at(LAST, "v_raw1_high", [P, PACK, HALF], F32))
+        load_values(1, 0, HALF, at(LAST, "v_raw1_low", [P, PACK, HALF], F32))
+        load_values(1, HALF, E, sb("v_raw1_high", [P, PACK, HALF], F32))
 
         def listed(window, slots):
             return window[:].indirect(offsets[:, slots.start // 16 : slots.stop // 16])
@@ -152,30 +153,29 @@ def tile_attend_ownlists_positions_kernel(
                 nc.tensor.transpose(fac_bank[:, j, :], fac_cols[:, g, j : j + 1].to_broadcast([P, P]), ident[:])
             fac_banks.append(fac_bank)
 
-        halves = [slice(0, HALF), slice(HALF, I)]
         early = 384
         pos_early = at(EXPS, "pos_early", [P, early], F32)
         nc.vector.tensor_copy(pos_early[:], listed(pos_all, slice(0, early)))
-        dist2 = sb("dist2", [P, I], F32)
+        dist2 = at(PICKED, "dist2", [P, I], F32)
         nc.scalar.activation(dist2[:, :early], pos_early[:], ACT.Square, bias=qpos_col[:], scale=-1.0)
         scores_low = sb("scores_low", [P, HALF], F32)
-        nc.vector.tensor_copy(scores_low[:], listed(scores, halves[0]))
+        nc.vector.tensor_copy(scores_low[:], listed(scores, slice(0, HALF)))
         neg_pos_late = sb("neg_pos_late", [P, I - early], F32)
         nc.vector.tensor_tensor(neg_pos_late[:], listed(pos_all, slice(early, I)), minus_ones[:], ALU.mult)
         scores_high = at(EXPS, "scores_high", [P, HALF], F32)
-        nc.scalar.activation(scores_high[:], listed(scores, halves[1]), ACT.Copy)
+        nc.scalar.activation(scores_high[:], listed(scores, slice(HALF, I)), ACT.Copy)
         nc.scalar.activation(dist2[:, early:], neg_pos_late[:], ACT.Square, bias=qpos_col[:], scale=1.0)
         costs = at(LISTED, "costs", [P, I], F32)
-        for slots, part in zip(halves, (scores_low, scores_high)):
+        for c0, c1 in ((0, FIRST), (FIRST, HALF), (HALF, I)):
             nc.vector.scalar_tensor_tensor(
-                out=costs[:, slots],
-                in0=dist2[:, slots],
+                out=costs[:, c0:c1],
+                in0=dist2[:, c0:c1],
                 scalar=slope_col[:],
-                in1=part[:],
+                in1=scores_low[:, c0:c1] if c0 < HALF else scores_high[:],
                 op0=ALU.mult,
                 op1=ALU.subtract,
             )
-        nc.scalar.activation(listed(cost_full, halves[0]), costs[:, halves[0]], ACT.Copy)
+        nc.scalar.activation(listed(cost_full, slice(0, FIRST)), costs[:, :FIRST], ACT.Copy)
 
         def cast_values(engine, g, c0, c1, dst):
             base = c0 // HALF * HALF
@@ -193,37 +193,39 @@ def tile_attend_ownlists_positions_kernel(
                 in_=src.rearrange("p e j -> p (e j)"),
             )
 
-        v_bf0 = at(PEN, "v_bf0", [P, E, PACK], BF16)
-        v_codes = [sb("v_codes0", [P, E], U32)]
         v_scales = [sb(f"v_scales{g}", [P, E], U8) for g in range(passes)]
-        cast_values("vector", 0, 0, HALF, v_bf0[:, :HALF, :])
+        v_bf_first = at(PEN, "v_bf_first", [P, QUARTER, PACK], BF16)
+        cast_values("vector", 0, 0, QUARTER, v_bf_first[:])
         least = sb("least", [P, 1], F32)
         nc.vector.tensor_reduce(least[:], costs[:], AXIS.X, ALU.min)
+        nc.vector.tensor_copy(listed(cost_full, slice(FIRST, I)), costs[:, FIRST:])
+        v_bf_rest = at(PICKED, "v_bf_rest", [P, E - QUARTER, PACK], BF16)
+        cast_values("scalar", 0, QUARTER, HALF, v_bf_rest[:, :QUARTER, :])
+        cast_values("pool", 0, HALF, E, v_bf_rest[:, QUARTER:, :])
         listed_exp = at(SUMMED, "listed_exp", [P, I], F32)
         row_sum = sb("row_sum", [P, 1], F32)
         nc.scalar.activation(listed_exp[:], costs[:], ACT.Exp, bias=least[:], scale=-1.0, accum_out=row_sum[:])
-        cast_values("vector", 0, HALF, E, v_bf0[:, HALF:, :])
-        nc.vector.tensor_copy(listed(cost_full, halves[1]), costs[:, halves[1]])
-        v_bf_low = at(RAW, "v_bf_low", [P, HALF, PACK], BF16)
-        cast_values("pool", 1, 0, BY_POOL, v_bf_low[:, :BY_POOL, :])
-        cast_values("scalar", 1, BY_POOL, HALF, v_bf_low[:, BY_POOL:, :])
-        v_bf_high = at(SUMMED, "v_bf_high", [P, HALF, PACK], BF16)
-        cast_values("scalar", 1, HALF, E, v_bf_high[:])
-        quantise_values(0, 0, E, v_bf0[:])
+        v_bf_second = at(SUMMED + 1024, "v_bf_second", [P, E - 64, PACK], BF16)
+        cast_values("pool", 1, 0, QUARTER, v_bf_second[:, :QUARTER, :])
+        cast_values("scalar", 1, QUARTER, HALF, v_bf_second[:, QUARTER:HALF, :])
+        cast_values("scalar", 1, HALF, E - 64, v_bf_second[:, HALF:, :])
         inv_sum = sb("inv_sum", [P, 1], F32)
         nc.vector.reciprocal(inv_sum[:], row_sum[:])
+        v_codes = [at(SUMMED - 1024, "v_codes0", [P, E], U32)]
+        quantise_values(0, 0, QUARTER, v_bf_first[:])
+        quantise_values(0, QUARTER, E, v_bf_rest[:])
 
         p_early = at(LAST + 1024, "p_early", [P, 3, HALF], F32)
         p_last = at(LAST, "p_last", [P, HALF], F32)
         w_t = []
         for g in range(passes):
-            w_bf = at(PEN + 1024 * g, f"w_bf{g}", [P, K_PASS], BF16)
+            w_bf = at(PEN + 1024 * (1 + g), f"w_bf{g}", [P, K_PASS], BF16)
             turned = bank(1 + g, f"turned{g}", [P, 2, Q])
             cost_pass = cost_full[:, g * K_PASS : (g + 1) * K_PASS].rearrange("q (p j) -> q p j", j=PACK)
             for u in range(2):
                 pair = w_bf[:, u * HALF : (u + 1) * HALF]
                 last = (g, u) == (passes - 1, 1)
-                cuts = (0, 3 * P // 4, P) if u else (0, P)
+                cuts = (0, 3 * P // 4, P) if u else (0, P) if g else (0, P // 2, P)
                 p_piece = p_last[:] if last else p_early[:, 2 * g + u, :]
                 for p0, p1 in zip(cuts, cuts[1:]):
                     p_pair = p_piece[:, 2 * p0 : 2 * p1].rearrange("q (p e) -> q p e", e=2)
@@ -242,8 +244,8 @@ def tile_attend_ownlists_positions_kernel(
             w_t.append((turned, sb(f"w_t{g}", [P, Q * PACK], BF16)))
 
         v_codes.append(at(LAST + 1024, "v_codes1", [P, E], U32))
-        quantise_values(1, 0, HALF, v_bf_low[:])
-        quantise_values(1, HALF, E, v_bf_high[:])
+        for c0, c1 in ((0, HALF), (HALF, HALF + QUARTER), (HALF + QUARTER, E - 64)):
+            quantise_values(1, c0, c1, v_bf_second[:, c0:c1, :])
 
         w_codes = []
         w_scales = []
@@ -264,6 +266,10 @@ def tile_attend_ownlists_positions_kernel(
                 )
             w_codes.append(codes)
             w_scales.append(scales)
+            if g == 0:
+                v_bf_late = at(PEN + 1024, "v_bf_late", [P, 64, PACK], BF16)
+                cast_values("scalar", 1, E - 64, E, v_bf_late[:])
+        quantise_values(1, E - 64, E, v_bf_late[:])
 
         pieces = list(range(0, E, P))
         out_banks = [bank(b, f"out_bank{c0}", [P, P]) for b, c0 in zip((6, 7, 0, 5), pieces)]

@@ -205,15 +205,17 @@ def tile_attend_ownlists_positions_kernel(
         listed_exp = at(SUMMED, "listed_exp", [P, I], F32)
         row_sum = sb("row_sum", [P, 1], F32)
         nc.scalar.activation(listed_exp[:], costs[:], ACT.Exp, bias=least[:], scale=-1.0, accum_out=row_sum[:])
-        v_bf_second = at(SUMMED + 1024, "v_bf_second", [P, E - 64, PACK], BF16)
-        cast_values("pool", 1, 0, QUARTER, v_bf_second[:, :QUARTER, :])
-        cast_values("scalar", 1, QUARTER, HALF, v_bf_second[:, QUARTER:HALF, :])
-        cast_values("scalar", 1, HALF, E - 64, v_bf_second[:, HALF:, :])
+        v_bf_second = at(SUMMED + 1024, "v_bf_second", [P, E - QUARTER, PACK], BF16)
+        cast_values("scalar", 1, 0, HALF, v_bf_second[:, :HALF, :])
+        cast_values("scalar", 1, HALF, E - QUARTER, v_bf_second[:, HALF:, :])
         inv_sum = sb("inv_sum", [P, 1], F32)
         nc.vector.reciprocal(inv_sum[:], row_sum[:])
         v_codes = [at(SUMMED - 1024, "v_codes0", [P, E], U32)]
         quantise_values(0, 0, QUARTER, v_bf_first[:])
-        quantise_values(0, QUARTER, E, v_bf_rest[:])
+        quantise_values(0, QUARTER, HALF, v_bf_rest[:, :QUARTER, :])
+        quantise_values(0, HALF, E, v_bf_rest[:, QUARTER:, :])
+        v_bf_last = at(PICKED, "v_bf_last", [P, QUARTER, PACK], BF16)
+        cast_values("pool", 1, E - QUARTER, E, v_bf_last[:])
 
         p_early = at(LAST + 1024, "p_early", [P, 3, HALF], F32)
         p_last = at(LAST, "p_last", [P, HALF], F32)
@@ -244,8 +246,9 @@ def tile_attend_ownlists_positions_kernel(
             w_t.append((turned, sb(f"w_t{g}", [P, Q * PACK], BF16)))
 
         v_codes.append(at(LAST + 1024, "v_codes1", [P, E], U32))
-        for c0, c1 in ((0, HALF), (HALF, HALF + QUARTER), (HALF + QUARTER, E - 64)):
+        for c0, c1 in ((0, HALF), (HALF, E - QUARTER)):
             quantise_values(1, c0, c1, v_bf_second[:, c0:c1, :])
+        quantise_values(1, E - QUARTER, E, v_bf_last[:])
 
         w_codes = []
         w_scales = []
@@ -266,10 +269,6 @@ def tile_attend_ownlists_positions_kernel(
                 )
             w_codes.append(codes)
             w_scales.append(scales)
-            if g == 0:
-                v_bf_late = at(PEN + 1024, "v_bf_late", [P, 64, PACK], BF16)
-                cast_values("scalar", 1, E - 64, E, v_bf_late[:])
-        quantise_values(1, E - 64, E, v_bf_late[:])
 
         pieces = list(range(0, E, P))
         out_banks = [bank(b, f"out_bank{c0}", [P, P]) for b, c0 in zip((6, 7, 0, 5), pieces)]

@@ -46,7 +46,7 @@ def tile_attend_ownlists_positions_kernel(
         def bank(n, name, shape):
             return psum.tile(shape, F32, name=name, tag=f"bank{n}")
 
-        PEN, EXPS, PICKED, IDENT, LISTED, SUMMED, LAST = 0, 4096, 8192, 12288, 12800, 16896, 22528
+        PEN, EXPS, PICKED, IDENT, LISTED, SUMMED, LAST, LOW = 0, 4096, 8192, 12288, 12800, 16896, 22528, 26624
 
         pos_cols = sb("pos_cols", [P, PACK], F32)
         nc.sync.dma_start(out=pos_cols[:], in_=pos[0:1, K_PASS:].rearrange("o (p j) -> p (o j)", j=PACK))
@@ -77,7 +77,7 @@ def tile_attend_ownlists_positions_kernel(
             )
 
         load_values(0, 0, HALF, sb("v_raw0_low", [P, PACK, HALF], F32))
-        load_values(0, HALF, E, sb("v_raw0_high", [P, PACK, HALF], F32))
+        load_values(0, HALF, E, at(LOW, "v_raw0_high", [P, PACK, HALF], F32))
         fac_cols = sb("fac_cols", [P, passes, PACK], F32)
         nc.sync.dma_start(out=fac_cols[:], in_=fac.rearrange("o (g p j) -> p (o g) j", g=passes, j=PACK))
         load_values(1, 0, HALF, at(LAST, "v_raw1_low", [P, PACK, HALF], F32))
@@ -202,12 +202,14 @@ def tile_attend_ownlists_positions_kernel(
         v_bf_rest = at(PICKED, "v_bf_rest", [P, E - QUARTER, PACK], BF16)
         cast_values("scalar", 0, QUARTER, HALF, v_bf_rest[:, :QUARTER, :])
         cast_values("pool", 0, HALF, E, v_bf_rest[:, QUARTER:, :])
+        v_bf_small = at(LOW, "v_bf_small", [P, 64, PACK], BF16)
+        cast_values("pool", 1, 0, 64, v_bf_small[:])
         listed_exp = at(SUMMED, "listed_exp", [P, I], F32)
         row_sum = sb("row_sum", [P, 1], F32)
         nc.scalar.activation(listed_exp[:], costs[:], ACT.Exp, bias=least[:], scale=-1.0, accum_out=row_sum[:])
-        v_bf_second = at(SUMMED + 1024, "v_bf_second", [P, E - QUARTER, PACK], BF16)
-        cast_values("scalar", 1, 0, HALF, v_bf_second[:, :HALF, :])
-        cast_values("scalar", 1, HALF, E - QUARTER, v_bf_second[:, HALF:, :])
+        v_bf_second = at(SUMMED + 1024, "v_bf_second", [P, HALF, PACK], BF16)
+        cast_values("scalar", 1, 64, HALF, v_bf_second[:, : HALF - 64, :])
+        cast_values("scalar", 1, HALF, HALF + 64, v_bf_second[:, HALF - 64 :, :])
         inv_sum = sb("inv_sum", [P, 1], F32)
         nc.vector.reciprocal(inv_sum[:], row_sum[:])
         v_codes = [at(SUMMED - 1024, "v_codes0", [P, E], U32)]
@@ -215,7 +217,7 @@ def tile_attend_ownlists_positions_kernel(
         quantise_values(0, QUARTER, HALF, v_bf_rest[:, :QUARTER, :])
         quantise_values(0, HALF, E, v_bf_rest[:, QUARTER:, :])
         v_bf_last = at(PICKED, "v_bf_last", [P, QUARTER, PACK], BF16)
-        cast_values("pool", 1, E - QUARTER, E, v_bf_last[:])
+        cast_values("pool", 1, HALF + 64, E - 64, v_bf_last[:])
 
         p_early = at(LAST + 1024, "p_early", [P, 3, HALF], F32)
         p_last = at(LAST, "p_last", [P, HALF], F32)
@@ -246,9 +248,9 @@ def tile_attend_ownlists_positions_kernel(
             w_t.append((turned, sb(f"w_t{g}", [P, Q * PACK], BF16)))
 
         v_codes.append(at(LAST + 1024, "v_codes1", [P, E], U32))
-        for c0, c1 in ((0, HALF), (HALF, E - QUARTER)):
-            quantise_values(1, c0, c1, v_bf_second[:, c0:c1, :])
-        quantise_values(1, E - QUARTER, E, v_bf_last[:])
+        quantise_values(1, 64, HALF + 64, v_bf_second[:])
+        quantise_values(1, 0, 64, v_bf_small[:])
+        quantise_values(1, HALF + 64, E - 64, v_bf_last[:])
 
         w_codes = []
         w_scales = []
@@ -269,6 +271,10 @@ def tile_attend_ownlists_positions_kernel(
                 )
             w_codes.append(codes)
             w_scales.append(scales)
+            if g == 0:
+                v_bf_late = at(PEN + 1024, "v_bf_late", [P, 64, PACK], BF16)
+                cast_values("scalar", 1, E - 64, E, v_bf_late[:])
+        quantise_values(1, E - 64, E, v_bf_late[:])
 
         pieces = list(range(0, E, P))
         out_banks = [bank(b, f"out_bank{c0}", [P, P]) for b, c0 in zip((6, 7, 0, 5), pieces)]

@@ -22,7 +22,8 @@ PACK = 4
 K_PASS = P * PACK
 HALF = 256
 QUARTER = 128
-FIRST = 160
+FIRST = 224
+BY_POOL = 192
 UNLISTED = 2.0**100
 
 
@@ -46,7 +47,7 @@ def tile_attend_ownlists_positions_kernel(
         def bank(n, name, shape):
             return psum.tile(shape, F32, name=name, tag=f"bank{n}")
 
-        PEN, EXPS, PICKED, IDENT, LISTED, SUMMED, LAST, LOW = 0, 4096, 8192, 12288, 12800, 16896, 22528, 26624
+        PEN, EXPS, PICKED, IDENT, LISTED, SUMMED = 0, 4096, 8192, 12288, 12800, 16896
 
         pos_cols = sb("pos_cols", [P, PACK], F32)
         nc.sync.dma_start(out=pos_cols[:], in_=pos[0:1, K_PASS:].rearrange("o (p j) -> p (o j)", j=PACK))
@@ -77,10 +78,10 @@ def tile_attend_ownlists_positions_kernel(
             )
 
         load_values(0, 0, HALF, sb("v_raw0_low", [P, PACK, HALF], F32))
-        load_values(0, HALF, E, at(LOW, "v_raw0_high", [P, PACK, HALF], F32))
+        load_values(0, HALF, E, sb("v_raw0_high", [P, PACK, HALF], F32))
         fac_cols = sb("fac_cols", [P, passes, PACK], F32)
         nc.sync.dma_start(out=fac_cols[:], in_=fac.rearrange("o (g p j) -> p (o g) j", g=passes, j=PACK))
-        load_values(1, 0, HALF, at(LAST, "v_raw1_low", [P, PACK, HALF], F32))
+        load_values(1, 0, HALF, sb("v_raw1_low", [P, PACK, HALF], F32))
         load_values(1, HALF, E, sb("v_raw1_high", [P, PACK, HALF], F32))
 
         def listed(window, slots):
@@ -194,36 +195,34 @@ def tile_attend_ownlists_positions_kernel(
             )
 
         v_scales = [sb(f"v_scales{g}", [P, E], U8) for g in range(passes)]
-        v_bf_first = at(PEN, "v_bf_first", [P, QUARTER, PACK], BF16)
-        cast_values("vector", 0, 0, QUARTER, v_bf_first[:])
+        v_bf_first = at(PEN, "v_bf_first", [P, E - QUARTER, PACK], BF16)
+        cast_values("vector", 0, 0, HALF, v_bf_first[:, :HALF, :])
+        cast_values("vector", 0, HALF, E - QUARTER, v_bf_first[:, HALF:, :])
         least = sb("least", [P, 1], F32)
         nc.vector.tensor_reduce(least[:], costs[:], AXIS.X, ALU.min)
         nc.vector.tensor_copy(listed(cost_full, slice(FIRST, I)), costs[:, FIRST:])
-        v_bf_rest = at(PICKED, "v_bf_rest", [P, E - QUARTER, PACK], BF16)
-        cast_values("scalar", 0, QUARTER, HALF, v_bf_rest[:, :QUARTER, :])
-        cast_values("pool", 0, HALF, E, v_bf_rest[:, QUARTER:, :])
-        v_bf_small = at(LOW, "v_bf_small", [P, 64, PACK], BF16)
-        cast_values("pool", 1, 0, 64, v_bf_small[:])
+        v_bf_rest = at(PICKED, "v_bf_rest", [P, QUARTER, PACK], BF16)
+        cast_values("scalar", 0, E - QUARTER, E, v_bf_rest[:])
+        v_bf_pool = sb("v_bf_pool", [P, BY_POOL, PACK], BF16)
+        cast_values("pool", 1, 0, BY_POOL, v_bf_pool[:])
         listed_exp = at(SUMMED, "listed_exp", [P, I], F32)
         row_sum = sb("row_sum", [P, 1], F32)
         nc.scalar.activation(listed_exp[:], costs[:], ACT.Exp, bias=least[:], scale=-1.0, accum_out=row_sum[:])
         v_bf_second = at(SUMMED + 1024, "v_bf_second", [P, HALF, PACK], BF16)
-        cast_values("scalar", 1, 64, HALF, v_bf_second[:, : HALF - 64, :])
-        cast_values("scalar", 1, HALF, HALF + 64, v_bf_second[:, HALF - 64 :, :])
+        cast_values("scalar", 1, BY_POOL, HALF, v_bf_second[:, : HALF - BY_POOL, :])
+        cast_values("scalar", 1, HALF, HALF + BY_POOL, v_bf_second[:, HALF - BY_POOL :, :])
         inv_sum = sb("inv_sum", [P, 1], F32)
         nc.vector.reciprocal(inv_sum[:], row_sum[:])
         v_codes = [at(SUMMED - 1024, "v_codes0", [P, E], U32)]
-        quantise_values(0, 0, QUARTER, v_bf_first[:])
-        quantise_values(0, QUARTER, HALF, v_bf_rest[:, :QUARTER, :])
-        quantise_values(0, HALF, E, v_bf_rest[:, QUARTER:, :])
-        v_bf_last = at(PICKED, "v_bf_last", [P, QUARTER, PACK], BF16)
-        cast_values("pool", 1, HALF + 64, E - 64, v_bf_last[:])
+        quantise_values(0, 0, HALF, v_bf_first[:, :HALF, :])
+        quantise_values(0, HALF, E - QUARTER, v_bf_first[:, HALF:, :])
+        quantise_values(0, E - QUARTER, E, v_bf_rest[:])
 
-        p_early = at(LAST + 1024, "p_early", [P, 3, HALF], F32)
-        p_last = at(LAST, "p_last", [P, HALF], F32)
+        p_early = at(LISTED - 2048, "p_early", [P, 3, HALF], F32)
+        p_last = at(LISTED + 1024, "p_last", [P, HALF], F32)
         w_t = []
         for g in range(passes):
-            w_bf = at(PEN + 1024 * (1 + g), f"w_bf{g}", [P, K_PASS], BF16)
+            w_bf = at(EXPS + 1024 * g, f"w_bf{g}", [P, K_PASS], BF16)
             turned = bank(1 + g, f"turned{g}", [P, 2, Q])
             cost_pass = cost_full[:, g * K_PASS : (g + 1) * K_PASS].rearrange("q (p j) -> q p j", j=PACK)
             for u in range(2):
@@ -247,10 +246,10 @@ def tile_attend_ownlists_positions_kernel(
                 nc.tensor.transpose(turned[:, u, :], pair.bitcast(F32), ident[:])
             w_t.append((turned, sb(f"w_t{g}", [P, Q * PACK], BF16)))
 
-        v_codes.append(at(LAST + 1024, "v_codes1", [P, E], U32))
-        quantise_values(1, 64, HALF + 64, v_bf_second[:])
-        quantise_values(1, 0, 64, v_bf_small[:])
-        quantise_values(1, HALF + 64, E - 64, v_bf_last[:])
+        v_codes.append(at(LISTED - 2048, "v_codes1", [P, E], U32))
+        quantise_values(1, 0, QUARTER, v_bf_pool[:, :QUARTER, :])
+        quantise_values(1, QUARTER, BY_POOL, v_bf_pool[:, QUARTER:, :])
+        quantise_values(1, BY_POOL, HALF + BY_POOL, v_bf_second[:])
 
         w_codes = []
         w_scales = []
@@ -272,7 +271,7 @@ def tile_attend_ownlists_positions_kernel(
             w_codes.append(codes)
             w_scales.append(scales)
             if g == 0:
-                v_bf_late = at(PEN + 1024, "v_bf_late", [P, 64, PACK], BF16)
+                v_bf_late = at(EXPS, "v_bf_late", [P, 64, PACK], BF16)
                 cast_values("scalar", 1, E - 64, E, v_bf_late[:])
         quantise_values(1, E - 64, E, v_bf_late[:])
 

@@ -23,7 +23,6 @@ K_PASS = P * PACK
 HALF = 256
 QUARTER = 128
 FIRST = 224
-BY_POOL = 192
 UNLISTED = 2.0**100
 
 
@@ -182,7 +181,7 @@ def tile_attend_ownlists_positions_kernel(
             base = c0 // HALF * HALF
             src = v_raw[g, base][:, :, c0 - base : c1 - base]
             if engine == "pool":
-                nc.gpsimd.tensor_copy(out=dst, in_=src.rearrange("p j e -> p e j"))
+                nc.gpsimd.tensor_scalar(dst, src.rearrange("p j e -> p e j"), 1.0, 0.0, ALU.mult, ALU.add)
             else:
                 copy = nc.scalar.copy if engine == "scalar" else nc.vector.tensor_copy
                 copy(out=dst.rearrange("p (c i) j -> p c j i", i=4), in_=src.rearrange("p j (c i) -> p c j i", i=4))
@@ -203,14 +202,13 @@ def tile_attend_ownlists_positions_kernel(
         nc.vector.tensor_copy(listed(cost_full, slice(FIRST, I)), costs[:, FIRST:])
         v_bf_rest = at(PICKED, "v_bf_rest", [P, QUARTER, PACK], BF16)
         cast_values("scalar", 0, E - QUARTER, E, v_bf_rest[:])
-        v_bf_pool = sb("v_bf_pool", [P, BY_POOL, PACK], BF16)
-        cast_values("pool", 1, 0, BY_POOL, v_bf_pool[:])
+        v_bf_pool = sb("v_bf_pool", [P, HALF, PACK], BF16)
+        cast_values("pool", 1, 0, HALF, v_bf_pool[:])
         listed_exp = at(SUMMED, "listed_exp", [P, I], F32)
         row_sum = sb("row_sum", [P, 1], F32)
         nc.scalar.activation(listed_exp[:], costs[:], ACT.Exp, bias=least[:], scale=-1.0, accum_out=row_sum[:])
-        v_bf_second = at(SUMMED + 1024, "v_bf_second", [P, HALF, PACK], BF16)
-        cast_values("scalar", 1, BY_POOL, HALF, v_bf_second[:, : HALF - BY_POOL, :])
-        cast_values("scalar", 1, HALF, HALF + BY_POOL, v_bf_second[:, HALF - BY_POOL :, :])
+        v_bf_second = at(SUMMED + 1024, "v_bf_second", [P, HALF - 64, PACK], BF16)
+        cast_values("scalar", 1, HALF, E - 64, v_bf_second[:])
         inv_sum = sb("inv_sum", [P, 1], F32)
         nc.vector.reciprocal(inv_sum[:], row_sum[:])
         v_codes = [at(SUMMED - 1024, "v_codes0", [P, E], U32)]
@@ -247,9 +245,9 @@ def tile_attend_ownlists_positions_kernel(
             w_t.append((turned, sb(f"w_t{g}", [P, Q * PACK], BF16)))
 
         v_codes.append(at(LISTED - 2048, "v_codes1", [P, E], U32))
-        quantise_values(1, 0, QUARTER, v_bf_pool[:, :QUARTER, :])
-        quantise_values(1, QUARTER, BY_POOL, v_bf_pool[:, QUARTER:, :])
-        quantise_values(1, BY_POOL, HALF + BY_POOL, v_bf_second[:])
+        quantise_values(1, 0, HALF, v_bf_pool[:])
+        quantise_values(1, HALF, E - QUARTER, v_bf_second[:, :QUARTER, :])
+        quantise_values(1, E - QUARTER, E - 64, v_bf_second[:, QUARTER:, :])
 
         w_codes = []
         w_scales = []

@@ -22,7 +22,7 @@ PACK = 4
 K_PASS = P * PACK
 HALF = 256
 QUARTER = 128
-FIRST = 224
+FIRST = 192
 UNLISTED = 2.0**100
 
 
@@ -194,14 +194,14 @@ def tile_attend_ownlists_positions_kernel(
             )
 
         v_scales = [sb(f"v_scales{g}", [P, E], U8) for g in range(passes)]
-        v_bf_first = at(PEN, "v_bf_first", [P, E - QUARTER, PACK], BF16)
-        cast_values("vector", 0, 0, HALF, v_bf_first[:, :HALF, :])
-        cast_values("vector", 0, HALF, E - QUARTER, v_bf_first[:, HALF:, :])
+        v_bf_first = at(PEN, "v_bf_first", [P, HALF, PACK], BF16)
+        cast_values("vector", 0, 0, HALF, v_bf_first[:])
+        v_bf_rest = at(PICKED, "v_bf_rest", [P, HALF, PACK], BF16)
+        cast_values("vector", 0, HALF, HALF + 64, v_bf_rest[:, :64, :])
         least = sb("least", [P, 1], F32)
         nc.vector.tensor_reduce(least[:], costs[:], AXIS.X, ALU.min)
         nc.vector.tensor_copy(listed(cost_full, slice(FIRST, I)), costs[:, FIRST:])
-        v_bf_rest = at(PICKED, "v_bf_rest", [P, QUARTER, PACK], BF16)
-        cast_values("scalar", 0, E - QUARTER, E, v_bf_rest[:])
+        cast_values("scalar", 0, HALF + 64, E, v_bf_rest[:, 64:, :])
         v_bf_pool = sb("v_bf_pool", [P, HALF, PACK], BF16)
         cast_values("pool", 1, 0, HALF, v_bf_pool[:])
         listed_exp = at(SUMMED, "listed_exp", [P, I], F32)
@@ -212,9 +212,8 @@ def tile_attend_ownlists_positions_kernel(
         inv_sum = sb("inv_sum", [P, 1], F32)
         nc.vector.reciprocal(inv_sum[:], row_sum[:])
         v_codes = [at(SUMMED - 1024, "v_codes0", [P, E], U32)]
-        quantise_values(0, 0, HALF, v_bf_first[:, :HALF, :])
-        quantise_values(0, HALF, E - QUARTER, v_bf_first[:, HALF:, :])
-        quantise_values(0, E - QUARTER, E, v_bf_rest[:])
+        quantise_values(0, 0, HALF, v_bf_first[:])
+        quantise_values(0, HALF, E, v_bf_rest[:])
 
         p_early = at(LISTED - 2048, "p_early", [P, 3, HALF], F32)
         p_last = at(LISTED + 1024, "p_last", [P, HALF], F32)

from contextlib import ExitStack

import concourse.mybir as mybir

D, T, Q, I, E = 512, 1024, 128, 512, 512
FLOPS = 2 * D * T * Q + 2 * T * Q * E

F32 = mybir.dt.float32
BF16 = mybir.dt.bfloat16
I32 = mybir.dt.int32
U32 = mybir.dt.uint32
U16 = mybir.dt.uint16
U8 = mybir.dt.uint8
FP8X4 = mybir.dt.float8_e4m3fn_x4
FP4X4 = mybir.dt.float4_e2m1fn_x4
ALU = mybir.AluOpType
ACT = mybir.ActivationFunctionType
AXIS = mybir.AxisListType

P = 128
PACK = 4
K_PASS = P * PACK
HALF = 256
QUARTER = 128
FIRST = 192
UNLISTED = 2.0**100


def tile_attend_ownlists_positions_kernel(
    tc, query, keys_words, keys_scales, pos, qpos, slope, fac, vals, offs, out
):
    nc = tc.nc
    passes = T // K_PASS

    with ExitStack() as ctx:
        keep = ctx.enter_context(tc.tile_pool(name="keep", bufs=1))
        laid = ctx.enter_context(tc.tile_pool(name="laid", bufs=1))
        psum = ctx.enter_context(tc.psum_pool(name="psum", bufs=1))

        def sb(name, shape, dtype):
            return keep.tile(shape, dtype, name=name, tag=name, align_bytes=64)

        def at(offset, name, shape, dtype):
            return laid.tile(shape, dtype, name=name, tag=name, align_bytes=64, offset=offset)

        def bank(n, name, shape):
            return psum.tile(shape, F32, name=name, tag=f"bank{n}")

        PEN, EXPS, PICKED, IDENT, LISTED, SUMMED = 0, 4096, 8192, 12288, 12800, 16896

        pos_cols = sb("pos_cols", [P, PACK], F32)
        nc.sync.dma_start(out=pos_cols[:], in_=pos[0:1, K_PASS:].rearrange("o (p j) -> p (o j)", j=PACK))
        q_raw = sb("q_raw", [P, PACK, Q], F32)
        nc.sync.dma_start(out=q_raw[:], in_=query.rearrange("(p j) q -> p j q", j=PACK))
        k_scales = sb("k_scales", [P, T], U8)
        for quad in range(4):
            nc.sync.dma_start(
                out=k_scales[32 * quad : 32 * quad + 4, :].bitcast(I32),
                in_=keys_scales[0, 4 * quad : 4 * quad + 4, :].bitcast(I32),
            )
        k_words = at(LISTED, "k_words", [P, 2 * T], U8)
        nc.sync.dma_start(out=k_words[:].bitcast(I32), in_=keys_words[0].bitcast(I32))
        pos_all = sb("pos_all", [P, T], F32)
        nc.sync.dma_start(out=pos_all[:, :K_PASS], in_=pos[:, :K_PASS])
        offsets = keep.tile([P, I // 16], U16)
        nc.sync.dma_start(offsets[:], offs)
        qpos_col = sb("qpos_col", [P, 1], F32)
        nc.sync.dma_start(out=qpos_col[:], in_=qpos)
        slope_col = sb("slope_col", [P, 1], F32)
        nc.sync.dma_start(out=slope_col[:], in_=slope)
        v_raw = {}

        def load_values(g, c0, c1, tile):
            v_raw[g, c0] = tile
            nc.sync.dma_start(
                out=tile[:], in_=vals[g * K_PASS : (g + 1) * K_PASS, c0:c1].rearrange("(p j) e -> p j e", j=PACK)
            )

        load_values(0, 0, HALF, sb("v_raw0_low", [P, PACK, HALF], F32))
        load_values(0, HALF, E, sb("v_raw0_high", [P, PACK, HALF], F32))
        fac_cols = sb("fac_cols", [P, passes, PACK], F32)
        nc.sync.dma_start(out=fac_cols[:], in_=fac.rearrange("o (g p j) -> p (o g) j", g=passes, j=PACK))
        load_values(1, 0, HALF, sb("v_raw1_low", [P, PACK, HALF], F32))
        load_values(1, HALF, E, sb("v_raw1_high", [P, PACK, HALF], F32))

        def listed(window, slots):
            return window[:].indirect(offsets[:, slots.start // 16 : slots.stop // 16])

        zeros = sb("zeros", [P, P], F32)
        nc.gpsimd.memset(zeros[:], 0.0)
        ident_first = at(IDENT, "ident_first", [P, P], F32)
        ident = sb("ident", [P, P], F32)
        for tile in (ident_first, ident):
            nc.gpsimd.affine_select(
                out=tile[:],
                in_=zeros[:],
                compare_op=ALU.not_equal,
                fill=1.0,
                base=0,
                pattern=[[-1, P]],
                channel_multiplier=1,
            )
        cost_full = sb("cost_full", [P, T], F32)
        nc.gpsimd.memset(cost_full[:], UNLISTED)
        minus_ones = sb("minus_ones", [P, P], F32)
        nc.gpsimd.memset(minus_ones[:], -1.0)

        pos_bank = bank(0, "pos_bank", [P, PACK, P])
        for j in range(PACK):
            nc.tensor.transpose(
                pos_bank[:, j, :], pos_cols[:, j : j + 1].to_broadcast([P, P]), (ident if j else ident_first)[:]
            )
        nc.scalar.activation(
            pos_all[:, K_PASS:].rearrange("q (p j) -> q p j", j=PACK), pos_bank[:].rearrange("q j p -> q p j"), ACT.Copy
        )

        q_bf = sb("q_bf", [P, Q, PACK], BF16)
        q_halves = [slice(0, Q // 2), slice(Q // 2, Q)]
        nc.vector.tensor_copy(out=q_bf[:, :64, :], in_=q_raw[:, :, :64].rearrange("p j q -> p q j"))
        nc.scalar.copy(
            out=q_bf[:, 64:, :].rearrange("p (c i) j -> p c j i", i=4),
            in_=q_raw[:, :, 64:].rearrange("p j (c i) -> p c j i", i=4),
        )
        q_codes = at(IDENT, "q_codes", [P, Q], U32)
        q_scales = sb("q_scales", [P, Q], U8)
        for rows in q_halves:
            nc.vector.quantize_mx(
                out=q_codes[:, rows].bitcast(FP8X4),
                scales=q_scales[:, rows],
                in_=q_bf[:, rows, :].rearrange("p q j -> p (q j)"),
            )

        scores = at(PEN, "scores", [P, T], F32)
        cuts = (0, 128, 384, 640, 896, T)
        for h, (t0, t1) in enumerate(zip(cuts, cuts[1:])):
            cols = slice(t0, t1)
            score_bank = bank(1 + h, f"score_bank{h}", [P, t1 - t0])
            nc.tensor.matmul_mx(
                out=score_bank[:],
                lhsT=q_codes[:].bitcast(FP8X4),
                lhsT_scale=q_scales[:],
                rhs=k_words[:, 2 * t0 : 2 * t1].bitcast(FP4X4),
                rhs_scale=k_scales[:, cols],
                start=True,
                stop=True,
            )
            nc.scalar.activation(scores[:, cols], score_bank[:], ACT.Copy)

        fac_banks = []
        for g in range(passes):
            fac_bank = bank(3 + g, f"fac_bank{g}", [P, PACK, P])
            for j in range(PACK):
                nc.tensor.transpose(fac_bank[:, j, :], fac_cols[:, g, j : j + 1].to_broadcast([P, P]), ident[:])
            fac_banks.append(fac_bank)

        early = 384
        pos_early = at(EXPS, "pos_early", [P, early], F32)
        nc.vector.tensor_copy(pos_early[:], listed(pos_all, slice(0, early)))
        dist2 = at(PICKED, "dist2", [P, I], F32)
        nc.scalar.activation(dist2[:, :early], pos_early[:], ACT.Square, bias=qpos_col[:], scale=-1.0)
        scores_low = sb("scores_low", [P, HALF], F32)
        nc.vector.tensor_copy(scores_low[:], listed(scores, slice(0, HALF)))
        neg_pos_late = sb("neg_pos_late", [P, I - early], F32)
        nc.vector.tensor_tensor(neg_pos_late[:], listed(pos_all, slice(early, I)), minus_ones[:], ALU.mult)
        scores_high = at(EXPS, "scores_high", [P, HALF], F32)
        nc.scalar.activation(scores_high[:], listed(scores, slice(HALF, I)), ACT.Copy)
        nc.scalar.activation(dist2[:, early:], neg_pos_late[:], ACT.Square, bias=qpos_col[:], scale=1.0)
        costs = at(LISTED, "costs", [P, I], F32)
        for c0, c1 in ((0, FIRST), (FIRST, HALF), (HALF, I)):
            nc.vector.scalar_tensor_tensor(
                out=costs[:, c0:c1],
                in0=dist2[:, c0:c1],
                scalar=slope_col[:],
                in1=scores_low[:, c0:c1] if c0 < HALF else scores_high[:],
                op0=ALU.mult,
                op1=ALU.subtract,
            )
        nc.scalar.activation(listed(cost_full, slice(0, FIRST)), costs[:, :FIRST], ACT.Copy)

        def cast_values(engine, g, c0, c1, dst):
            base = c0 // HALF * HALF
            src = v_raw[g, base][:, :, c0 - base : c1 - base]
            if engine == "pool":
                nc.gpsimd.tensor_scalar(dst, src.rearrange("p j e -> p e j"), 1.0, 0.0, ALU.mult, ALU.add)
            else:
                copy = nc.scalar.copy if engine == "scalar" else nc.vector.tensor_copy
                copy(out=dst.rearrange("p (c i) j -> p c j i", i=4), in_=src.rearrange("p j (c i) -> p c j i", i=4))

        def quantise_values(g, c0, c1, src):
            nc.vector.quantize_mx(
                out=v_codes[g][:, c0:c1].bitcast(FP8X4),
                scales=v_scales[g][:, c0:c1],
                in_=src.rearrange("p e j -> p (e j)"),
            )

        v_scales = [sb(f"v_scales{g}", [P, E], U8) for g in range(passes)]
        v_bf_first = at(PEN, "v_bf_first", [P, HALF, PACK], BF16)
        cast_values("vector", 0, 0, HALF, v_bf_first[:])
        v_bf_rest = at(PICKED, "v_bf_rest", [P, HALF, PACK], BF16)
        cast_values("vector", 0, HALF, HALF + 64, v_bf_rest[:, :64, :])
        least = sb("least", [P, 1], F32)
        nc.vector.tensor_reduce(least[:], costs[:], AXIS.X, ALU.min)
        nc.vector.tensor_copy(listed(cost_full, slice(FIRST, I)), costs[:, FIRST:])
        cast_values("scalar", 0, HALF + 64, E, v_bf_rest[:, 64:, :])
        v_bf_pool = sb("v_bf_pool", [P, HALF, PACK], BF16)
        cast_values("pool", 1, 0, HALF, v_bf_pool[:])
        listed_exp = at(SUMMED, "listed_exp", [P, I], F32)
        row_sum = sb("row_sum", [P, 1], F32)
        nc.scalar.activation(listed_exp[:], costs[:], ACT.Exp, bias=least[:], scale=-1.0, accum_out=row_sum[:])
        v_bf_second = at(SUMMED + 1024, "v_bf_second", [P, HALF - 64, PACK], BF16)
        cast_values("scalar", 1, HALF, E - 64, v_bf_second[:])
        inv_sum = sb("inv_sum", [P, 1], F32)
        nc.vector.reciprocal(inv_sum[:], row_sum[:])
        v_codes = [at(SUMMED - 1024, "v_codes0", [P, E], U32)]
        quantise_values(0, 0, HALF, v_bf_first[:])
        quantise_values(0, HALF, E, v_bf_rest[:])

        p_early = at(LISTED - 2048, "p_early", [P, 3, HALF], F32)
        p_last = at(LISTED + 1024, "p_last", [P, HALF], F32)
        w_t = []
        for g in range(passes):
            w_bf = at(EXPS + 1024 * g, f"w_bf{g}", [P, K_PASS], BF16)
            turned = bank(1 + g, f"turned{g}", [P, 2, Q])
            cost_pass = cost_full[:, g * K_PASS : (g + 1) * K_PASS].rearrange("q (p j) -> q p j", j=PACK)
            for u in range(2):
                pair = w_bf[:, u * HALF : (u + 1) * HALF]
                last = (g, u) == (passes - 1, 1)
                cuts = (0, 3 * P // 4, P) if u else (0, P) if g else (0, P // 2, P)
                p_piece = p_last[:] if last else p_early[:, 2 * g + u, :]
                for p0, p1 in zip(cuts, cuts[1:]):
                    p_pair = p_piece[:, 2 * p0 : 2 * p1].rearrange("q (p e) -> q p e", e=2)
                    nc.scalar.activation(
                        p_pair, cost_pass[:, p0:p1, 2 * u : 2 * u + 2], ACT.Exp, bias=least[:], scale=-1.0
                    )
                    nc.vector.scalar_tensor_tensor(
                        out=pair[:, 2 * p0 : 2 * p1].rearrange("q (p e) -> q p e", e=2),
                        in0=p_pair,
                        scalar=inv_sum[:],
                        in1=fac_banks[g][:, 2 * u : 2 * u + 2, p0:p1].rearrange("q e p -> q p e"),
                        op0=ALU.mult,
                        op1=ALU.mult,
                    )
                nc.tensor.transpose(turned[:, u, :], pair.bitcast(F32), ident[:])
            w_t.append((turned, sb(f"w_t{g}", [P, Q * PACK], BF16)))

        v_codes.append(at(LISTED - 2048, "v_codes1", [P, E], U32))
        quantise_values(1, 0, HALF, v_bf_pool[:])
        quantise_values(1, HALF, E - QUARTER, v_bf_second[:, :QUARTER, :])
        quantise_values(1, E - QUARTER, E - 64, v_bf_second[:, QUARTER:, :])

        w_codes = []
        w_scales = []
        for g in range(passes):
            turned, w_tg = w_t[g]
            for rows in q_halves:
                nc.scalar.copy(
                    out=w_tg[:].bitcast(F32).rearrange("p (q u) -> p q u", u=2)[:, rows, :],
                    in_=turned[:, :, rows].rearrange("p u q -> p q u"),
                )
            codes = sb(f"w_codes{g}", [P, Q], U32)
            scales = sb(f"w_scales{g}", [P, Q], U8)
            for rows in q_halves:
                nc.vector.quantize_mx(
                    out=codes[:, rows].bitcast(FP8X4),
                    scales=scales[:, rows],
                    in_=w_tg[:, rows.start * PACK : rows.stop * PACK],
                )
            w_codes.append(codes)
            w_scales.append(scales)
            if g == 0:
                v_bf_late = at(EXPS, "v_bf_late", [P, 64, PACK], BF16)
                cast_values("scalar", 1, E - 64, E, v_bf_late[:])
        quantise_values(1, E - 64, E, v_bf_late[:])

        pieces = list(range(0, E, P))
        out_banks = [bank(b, f"out_bank{c0}", [P, P]) for b, c0 in zip((6, 7, 0, 5), pieces)]
        for g in range(passes):
            for out_bank, c0 in zip(out_banks, pieces):
                nc.tensor.matmul_mx(
                    out=out_bank[:],
                    lhsT=w_codes[g][:].bitcast(FP8X4),
                    lhsT_scale=w_scales[g][:],
                    rhs=v_codes[g][:, c0 : c0 + P].bitcast(FP8X4),
                    rhs_scale=v_scales[g][:, c0 : c0 + P],
                    start=(g == 0),
                    stop=(g == passes - 1),
                )
        result = sb("result", [P, E], F32)
        for n, (out_bank, c0) in enumerate(zip(out_banks, pieces)):
            if n % 2 == 0:
                nc.scalar.copy(out=result[:, c0 : c0 + P], in_=out_bank[:])
            else:
                nc.vector.tensor_copy(out=result[:, c0 : c0 + P], in_=out_bank[:])
            (nc.scalar, nc.sync)[n % 2].dma_start(out=out[:, c0 : c0 + P], in_=result[:, c0 : c0 + P])
